import numpy as np
import ml_dtypes


def mxq(x, axis, fmt="e4m3"):
    dtype, down = {"e4m3": (ml_dtypes.float8_e4m3fn, 7), "e5m2": (ml_dtypes.float8_e5m2, 14)}[fmt]
    v = np.moveaxis(np.asarray(x, np.float32).astype(ml_dtypes.bfloat16).astype(np.float64), axis, -1)
    blocks = v.reshape(v.shape[:-1] + (-1, 32))
    amax = np.abs(blocks).max(-1, keepdims=True)
    byte = np.maximum(np.where(amax > 0, np.frexp(amax)[1] - 1 + 127, 0) - down, 1)
    scale = np.exp2(byte - 127.0)
    codes = (blocks / scale).astype(np.float32).astype(dtype).astype(np.float64)
    return np.moveaxis((codes * scale).reshape(v.shape), -1, axis)


WIDE = False


def mx_kscale(k):
    if not WIDE:
        return np.ones(k)
    levels = np.array([10, -10, 5, -5, 0])
    if k % 512:
        return np.exp2(np.random.permutation(np.resize(levels, k // 32))).repeat(32)
    a = np.empty((k // 512, 16))
    for p in range(k // 512):
        a[p, :8] = np.random.permutation(np.resize(levels, 8))
        for g in range(8):
            far = levels[np.abs(levels - a[p, g]) >= 10]
            a[p, g + 8] = far[np.random.randint(len(far))]
    return np.exp2(a.ravel()).repeat(32)


def f64(x):
    return np.asarray(x).astype(np.float64)


def striped(idx):
    return np.tile(idx.reshape(-1, 16).T, (8, 1)).astype(np.uint16)


def unstriped(offs):
    return offs[:16].T.reshape(-1).astype(np.int64)


E2M1 = np.array([0.0, 0.5, 1.0, 1.5, 2.0, 3.0, 4.0, 6.0, -0.0, -0.5, -1.0, -1.5, -2.0, -3.0, -4.0, -6.0])


def pack_weight(w, fmt):
    k, n = w.shape
    w = f64(np.asarray(w, np.float32).astype(ml_dtypes.bfloat16)).reshape(k // 32, 32, n)
    amax = np.abs(w).max(1)
    if fmt == "e4m3":
        byte = np.frexp(amax)[1] - 1 + 127 - 7
    else:
        mant, ex = np.frexp(amax / 6.0)
        byte = np.where(mant > 0.5, ex, ex - 1) + 127
    byte = np.clip(np.where(amax > 0, byte, 1), 1, 254)
    scaled = (w * np.exp2(127.0 - byte)[:, None, :]).reshape(k, n).astype(np.float32)
    by_word = np.ascontiguousarray(scaled.reshape(k // 512, 128, 4, n).transpose(0, 1, 3, 2))
    if fmt == "e4m3":
        words = by_word.astype(ml_dtypes.float8_e4m3fn).view(np.uint8)
    else:
        c = by_word.astype(ml_dtypes.float4_e2m1fn).view(np.uint8) & 0xF
        words = (c[..., 0::2] | (c[..., 1::2] << 4)).reshape(k // 512, 128, 2 * n)
    return np.ascontiguousarray(words), np.ascontiguousarray(byte.astype(np.uint8).reshape(k // 512, 16, n))


def unpack_weight(words, scales, fmt):
    g, _, n = scales.shape
    words = np.ascontiguousarray(words).reshape(g, 128, n, -1)
    if fmt == "e4m3":
        vals = words.view(ml_dtypes.float8_e4m3fn).astype(np.float64)
    else:
        nib = np.empty((g, 128, n, 4), np.uint8)
        nib[..., 0::2] = words & 0xF
        nib[..., 1::2] = words >> 4
        vals = E2M1[nib]
    vals = vals * np.repeat(np.exp2(scales.astype(np.float64) - 127.0), 8, axis=1)[..., None]
    return vals.transpose(0, 1, 3, 2).reshape(g * 512, n)


def gelu(v):
    return 0.5 * v * (1.0 + np.tanh(np.sqrt(2.0 / np.pi) * (v + 0.044715 * v**3)))


K, T, S, T2, H, N = 1024, 2048, 512, 1024, 1024, 512

def setup_inputs():
    n = np.random.standard_normal
    s = mx_kscale(K)[:, None]
    u = mx_kscale(H)[:, None]
    tab_words, tab_scales = pack_weight(n((K, T)) * s, "e4m3")
    tab2_words, tab2_scales = pack_weight(n((K, T)) * s, "e4m3")
    w2_words, w2_scales = pack_weight(n((K, H)) / np.sqrt(K) / s, "e2m1")
    w3_words, w3_scales = pack_weight(n((K, H)) / np.sqrt(K) / s, "e4m3")
    perm = np.random.permutation(T2)
    return {
        "tab_words": tab_words, "tab_scales": tab_scales,
        "tab2_words": tab2_words, "tab2_scales": tab2_scales,
        "offs": striped(np.random.permutation(T)[:S]),
        "offs2": striped(np.random.permutation(T)[:S]),
        "offs3": striped(perm[:S]), "offs4": striped(perm[S:]),
        "w1": (1.5 * n((K, H)) / np.sqrt(K) / s).astype(np.float32),
        "w2_words": w2_words, "w2_scales": w2_scales,
        "w3_words": w3_words, "w3_scales": w3_scales,
        "w4": (0.7 * n((K, H)) / np.sqrt(K) / s).astype(np.float32),
        "wg1": np.exp(0.3 * n((128, S))).astype(np.float32),
        "wg2": np.exp(0.3 * n((128, S))).astype(np.float32),
        "gain": (np.random.uniform(0.5, 2.0, H) * u[:, 0]).astype(np.float32),
        "wo": (n((H, N)) / np.sqrt(H) / u).astype(np.float32),
    }

def reference(tab_words, tab_scales, tab2_words, tab2_scales, offs, offs2, offs3, offs4,
              w1, w2_words, w2_scales, w3_words, w3_scales, w4, wg1, wg2, gain, wo):
    v = unpack_weight(tab_words, tab_scales, "e4m3")[:, unstriped(offs)]
    v2 = unpack_weight(tab2_words, tab2_scales, "e4m3")[:, unstriped(offs2)]
    drive = mxq(f64(w1), 0, "e4m3").T @ v
    shear = unpack_weight(w2_words, w2_scales, "e2m1").T @ v
    h1 = drive / (1.0 + np.square(shear))
    h2 = (unpack_weight(w3_words, w3_scales, "e4m3").T @ v2) - (mxq(f64(w4), 0, "e4m3").T @ v)
    page = np.zeros((H, T2))
    page[:, unstriped(offs3)] = np.tile(f64(wg1), (H // 128, 1)) * h1
    page[:, unstriped(offs4)] = np.tile(f64(wg2), (H // 128, 1)) * h2
    z = np.tanh(page) * f64(gain)[:, None]
    return mxq(f64(wo), 0, "e4m3").T @ mxq(z, 0, "e4m3")

@@ -1,0 +1,359 @@
+from contextlib import ExitStack
+
+import concourse.mybir as mybir
+from concourse.masks import make_identity
+
+K, T, S, T2, H, N = 1024, 2048, 512, 1024, 1024, 512
+FLOPS = 2 * (4 * K * H * S + H * N * T2)
+
+F32 = mybir.dt.float32
+BF16 = mybir.dt.bfloat16
+I32 = mybir.dt.int32
+U32 = mybir.dt.uint32
+U16 = mybir.dt.uint16
+U8 = mybir.dt.uint8
+FP8X4 = mybir.dt.float8_e4m3fn_x4
+FP4X4 = mybir.dt.float4_e2m1fn_x4
+ACT = mybir.ActivationFunctionType
+MULT = mybir.AluOpType.mult
+
+P = 128
+PACK = 4
+PASS = P * PACK
+QUADS = 4
+HALVES = 2
+CHUNK = 256
+
+
+def tile_list_tokamak_edge_weave_kernel(
+    tc, tab_words, tab_scales, tab2_words, tab2_scales, offs, offs2, offs3, offs4,
+    w1, w2_words, w2_scales, w3_words, w3_scales, w4, wg1, wg2, gain, wo, out,
+):
+    nc = tc.nc
+    with ExitStack() as ctx:
+        lists = ctx.enter_context(tc.tile_pool(name="lists", bufs=1))
+        keep = ctx.enter_context(tc.tile_pool(name="keep", bufs=1))
+        psum = ctx.enter_context(tc.psum_pool(name="psum", bufs=1))
+
+        def sb(name, shape, dtype, tag=None, bufs=1):
+            return keep.tile(shape, dtype, name=name, tag=tag or name, bufs=bufs, align_bytes=64)
+
+        banks = [psum.tile([P, PASS], F32, name="bank%d" % b) for b in range(8)]
+
+        def bank(b):
+            return banks[b]
+
+        raw_ring = [sb("raw%d" % i, [P, PACK, PASS], F32) for i in range(4)]
+        grouped_ring = [sb("grouped%d" % i, [P, PACK * PASS], BF16) for i in range(4)]
+        stream = [sb("stream%d" % i, [P, S], F32) for i in range(4)]
+        damp_ring = [sb("damp%d" % i, [P, S], F32) for i in range(6)]
+        page_ring = [sb("page%d" % i, [P, T2], F32) for i in range(6)]
+
+        def load_list(name, src):
+            tile = lists.tile([P, S // 16], U16, name=name)
+            nc.sync.dma_start(tile[:], src)
+            return tile
+
+        def load_table_words(name, words, a):
+            tile = sb(name, [P, T], U32, tag="table%d" % a)
+            nc.sync.dma_start(tile[:].bitcast(I32), words[a].rearrange("p n i -> p (n i)").bitcast(I32))
+            return tile
+
+        def load_scales_side_by_side(tile, scales):
+            for q in range(QUADS):
+                nc.sync.dma_start(
+                    tile[32 * q : 32 * q + 4, :].bitcast(I32).rearrange("r (a n) -> r a n", a=2),
+                    scales[:, 4 * q : 4 * q + 4, :].bitcast(I32).rearrange("a r n -> r a n"),
+                )
+
+        def load_scales_stacked(tile, scales):
+            for q in range(QUADS):
+                nc.sync.dma_start(
+                    tile[32 * q : 32 * q + 8, :].bitcast(I32),
+                    scales[:, 4 * q : 4 * q + 4, :].bitcast(I32),
+                )
+
+        def load_rows(slot, w, a, cols):
+            raw = raw_ring[slot]
+            nc.sync.dma_start(raw[:], w[PASS * a : PASS * (a + 1), cols].rearrange("(p j) c -> p j c", j=PACK))
+            return raw
+
+        def load_cell_weights(name, wg):
+            tile = sb(name, [P, PACK, S], F32)
+            for q in range(QUADS):
+                nc.sync.dma_start(tile[32 * q : 32 * (q + 1), :, :], wg.rearrange("(q t) j -> q t j", t=PACK))
+            return tile
+
+        def gather(name, window, offsets, dtype):
+            picked = sb(name, [P, S], dtype)
+            nc.vector.tensor_copy(picked[:], window.indirect(offsets[:]))
+            return picked
+
+        def quantize(name, grouped, codes=None, scales=None):
+            if codes is None:
+                codes = sb(name + "_codes", [P, PASS], U32)[:]
+                scales = sb(name + "_scales", [P, PASS], U8)[:]
+            nc.vector.quantize_mx(out=codes.bitcast(FP8X4), scales=scales, in_=grouped)
+            return codes, scales
+
+        def first_stage_views(slot, raw):
+            grouped = grouped_ring[slot]
+            dst = grouped[:].rearrange("p (t m j) -> p m j t", t=PACK, j=PACK)
+            src = raw[:].rearrange("p j (m t) -> p m j t", t=PACK)
+            return grouped, dst, src
+
+        def mm(acc, lhs, lhs_s, rhs, rhs_s, start, stop):
+            nc.tensor.matmul_mx(out=acc, lhsT=lhs, lhsT_scale=lhs_s, rhs=rhs, rhs_scale=rhs_s, start=start, stop=stop)
+
+        half_cols = [slice(PASS * b, PASS * (b + 1)) for b in range(HALVES)]
+        col128 = [slice(P * t, P * (t + 1)) for t in range(PACK)]
+
+        tab_sc = sb("tab_sc", [P, 2 * T], U8)
+        w2_sc = sb("w2_sc", [P, 2 * H], U8)
+        tab2_sc = sb("tab2_sc", [P, T], U8)
+        w3_sc = sb("w3_sc", [P, H], U8)
+        nc.vector.memset(tab_sc[:].bitcast(I32), 0)
+        nc.vector.memset(w2_sc[:].bitcast(I32), 0)
+        nc.vector.memset(tab2_sc[:].bitcast(I32), 0)
+        nc.vector.memset(w3_sc[:].bitcast(I32), 0)
+        ident = sb("ident", [P, P], F32)
+        make_identity(nc, ident[:])
+        warm = sb("warm", [P, 1], F32)
+        nc.scalar.activation(warm[:], ident[:, 0:1], ACT.Abs_reciprocal_sqrt, bias=1.0)
+
+        idx = load_list("idx", offs)
+        load_scales_side_by_side(tab_sc, tab_scales)
+        tab = [load_table_words("tab%d" % a, tab_words, a) for a in range(2)]
+        load_scales_side_by_side(w2_sc, w2_scales)
+        w2c = []
+
+        def load_w2(b, tag):
+            w2c.append(sb("w2c%d" % b, [P, 2, 2 * PASS], U8, tag=tag))
+            nc.sync.dma_start(
+                w2c[b][:].bitcast(I32),
+                w2_words[:, :, 2 * PASS * b : 2 * PASS * (b + 1)].bitcast(I32).rearrange("a p n -> p a n"),
+            )
+
+        load_w2(0, "w2c0")
+        w1_raw0 = load_rows(0, w1, 0, half_cols[0])
+        w1_late = []
+        for h in range(2):
+            piece = sb("w1_late%d" % h, [P, PACK, PASS // 2], F32)
+            nc.sync.dma_start(
+                piece[:], w1[PASS : 2 * PASS, PASS // 2 * h : PASS // 2 * (h + 1)].rearrange("(p j) c -> p j c", j=PACK)
+            )
+            w1_late.append(piece)
+        idx3 = load_list("idx3", offs3)
+        wg1_sb = load_cell_weights("wg1_sb", wg1)
+
+        v, v_sc = [], []
+        for a in range(2):
+            v_sc.append(gather("v_sc%d" % a, tab_sc[:, T * a : T * (a + 1)], idx, U8))
+            v.append(gather("v%d" % a, tab[a][:], idx, U32))
+
+        idx2 = load_list("idx2", offs2)
+        load_scales_stacked(tab2_sc, tab2_scales)
+        tab2 = [load_table_words("tab2_%d" % a, tab2_words, a) for a in range(2)]
+        load_scales_stacked(w3_sc, w3_scales)
+        w3_raw = sb("w3_raw", [P, 2, H], I32)
+        nc.sync.dma_start(w3_raw[:], w3_words.rearrange("a p c i -> p a (c i)").bitcast(I32))
+        w4_raw = [load_rows(2 + a, w4, a, half_cols[0]) for a in range(2)]
+        idx4 = load_list("idx4", offs4)
+        wg2_sb = load_cell_weights("wg2_sb", wg2)
+        gain_sb = sb("gain_sb", [P, HALVES, PACK], F32)
+        nc.sync.dma_start(gain_sb[:], gain.rearrange("(b p t) -> p b t", b=HALVES, t=PACK))
+
+        root = sb("root", [P, PACK, PACK, P], F32)
+
+        def shear(b):
+            for a in range(2):
+                for c in range(PACK):
+                    mm(bank(c)[:], v[a][:, col128[c]].bitcast(FP8X4), v_sc[a][:, col128[c]],
+                       w2c[b][:, a, :].bitcast(FP4X4),
+                       w2_sc[:, H * a + PASS * b : H * a + PASS * (b + 1)], a == 0, a == 1)
+
+        def square_shear(ts):
+            for c in range(PACK):
+                nc.scalar.activation(
+                    root[:, ts, c, :], bank(c)[:].rearrange("p (m t) -> p t m", t=PACK)[:, ts, :], ACT.Square
+                )
+
+        def damping(b, t, turned):
+            flat = root[:, t, :, :]
+            nc.scalar.activation(flat, flat, ACT.Abs_reciprocal_sqrt, bias=1.0)
+            for c in range(PACK):
+                nc.tensor.transpose(turned[:, col128[c]], root[:, t, c, :], ident[:])
+            damp = damp_ring[(PACK * b + t) % 6]
+            nc.scalar.activation(damp[:], turned[:], ACT.Square)
+            return damp
+
+        def drive(w1q, damp, t, h1):
+            acc = bank(4 + t)
+            for a in range(2):
+                mm(acc[:], w1q[a][0][:, col128[t]].bitcast(FP8X4), w1q[a][1][:, col128[t]],
+                   v[a][:].bitcast(FP8X4), v_sc[a][:], a == 0, a == 1)
+            nc.vector.tensor_tensor(h1, acc[:], damp[:], MULT)
+
+        def put_drive(page, h1, t):
+            nc.vector.tensor_tensor(page[:].indirect(idx3[:]), h1, wg1_sb[:, t, :], MULT)
+
+        def cast_first_stage(name, slot, raw, scale):
+            grouped, dst, src = first_stage_views(slot, raw)
+            nc.scalar.activation(dst, src, ACT.Copy, scale=scale)
+            return quantize(name, grouped[:])
+
+        pages = [[page_ring[(PACK * b + t) % 6] for t in range(PACK)] for b in range(HALVES)]
+        shear(0)
+        square_shear(slice(0, 1))
+        damp0 = [damping(0, 0, bank(7))]
+        square_shear(slice(1, PACK))
+
+        grouped, dst, src = first_stage_views(0, w1_raw0)
+        nc.vector.tensor_copy(dst, src)
+        w1q = [quantize("w1_00", grouped[:])]
+        grouped = grouped_ring[1]
+        for h in range(2):
+            nc.vector.tensor_copy(
+                grouped[:].rearrange("p (t m j) -> p m j t", t=PACK, j=PACK)[:, P // 2 * h : P // 2 * (h + 1), :, :],
+                w1_late[h][:].rearrange("p j (m t) -> p m j t", t=PACK),
+            )
+        codes = sb("w1_01_codes", [P, PASS], U32)
+        scales = sb("w1_01_scales", [P, PASS], U8)
+        for lo, hi in ((0, 1), (1, 2), (2, 4)):
+            quantize(None, grouped[:, PASS * lo : PASS * hi], codes[:, P * lo : P * hi], scales[:, P * lo : P * hi])
+        w1q.append((codes[:], scales[:]))
+        for t in range(PACK - 1):
+            drive(w1q, damp0[t], t, stream[t % 2][:])
+            damp0.append(damping(0, t + 1, bank(4 + t)))
+            put_drive(pages[0][t], stream[t % 2][:], t)
+
+        load_w2(1, "w1_late0")
+        shear(1)
+        square_shear(slice(0, PACK))
+
+        v2_sc = gather("v2_sc", tab2_sc[:], idx2, U8)
+        v2 = [gather("v2_%d" % a, tab2[a][:], idx2, U32) for a in range(2)]
+
+        def order_w3(b):
+            codes = sb("w3c%d" % b, [P, 2, PASS], I32)
+            nc.vector.tensor_copy(
+                codes[:].rearrange("p a (t m) -> p a m t", t=PACK),
+                w3_raw[:, :, half_cols[b]].rearrange("p a (m t) -> p a m t", t=PACK),
+            )
+            scales = sb("w3s%d" % b, [P, PASS], U8)
+            nc.vector.tensor_copy(
+                scales[:].rearrange("p (t m) -> p m t", t=PACK),
+                w3_sc[:, half_cols[b]].rearrange("p (m t) -> p m t", t=PACK),
+            )
+            return codes, scales
+
+        def exchange(w3q, w4q, t):
+            acc = bank(t)
+            for a in range(2):
+                mm(acc[:], w3q[0][:, a, col128[t]].bitcast(FP8X4), w3q[1][4 * a : P, col128[t]],
+                   v2[a][:].bitcast(FP8X4), v2_sc[4 * a : P, :], a == 0, False)
+            for a in range(2):
+                mm(acc[:], w4q[a][0][:, col128[t]].bitcast(FP8X4), w4q[a][1][:, col128[t]],
+                   v[a][:].bitcast(FP8X4), v_sc[a][:], False, a == 1)
+            nc.scalar.copy(stream[t][:], acc[:])
+
+        def put_exchange(page, t):
+            nc.vector.tensor_tensor(page[:].indirect(idx4[:]), stream[t][:], wg2_sb[:, t, :], MULT)
+
+        z_pairs = sb("z_pairs", [P, PACK * T2], BF16)
+        z_slots = z_pairs[:].rearrange("p (c u m e) -> p u e c m", u=2, e=2, m=CHUNK)
+        z_words = z_pairs[:].bitcast(F32)
+        th = sb("th", [P, T2], F32)
+
+        def activate(page, b, t, chunks):
+            cols = slice(CHUNK * chunks.start, CHUNK * chunks.stop)
+            nc.scalar.activation(th[:, cols], page[:, cols], ACT.Tanh)
+            nc.scalar.activation(
+                z_slots[:, t // 2, t % 2, chunks, :], th[:, cols].rearrange("p (c m) -> p c m", m=CHUNK),
+                ACT.Copy, scale=gain_sb[:, b, t : t + 1],
+            )
+
+        def weave_views(grouped, chunk):
+            dst = grouped.bitcast(F32).rearrange("p (c i u) -> p c u i", i=4, u=2)
+            src = z_words[:, 2 * CHUNK * chunk : 2 * CHUNK * (chunk + 1)].rearrange("p (u c i) -> p c u i", i=4, u=2)
+            return dst, src
+
+        w3q = order_w3(0)
+        w4q = [cast_first_stage("w4_0%d" % a, 2 + a, w4_raw[a], -1.0) for a in range(2)]
+        damp1 = [damping(1, t, bank(t)) for t in range(PACK)]
+        held = grouped_ring[3][:, 0 : 2 * S].bitcast(F32)
+        drive(w1q, damp0[PACK - 1], PACK - 1, held)
+        put_drive(pages[0][PACK - 1], held, PACK - 1)
+
+        w1_raw = [load_rows(a, w1, a, half_cols[1]) for a in range(2)]
+        w4_raw = [load_rows(2 + a, w4, a, half_cols[1]) for a in range(2)]
+        w1q = [cast_first_stage("w1_1%d" % a, a, w1_raw[a], 1.0) for a in range(2)]
+        wo_raw = [load_rows(b, wo, b, slice(0, N)) for b in range(HALVES)]
+
+        for t in range(PACK):
+            exchange(w3q, w4q, t)
+        for t in range(PACK):
+            put_exchange(pages[0][t], t)
+        w4q = [cast_first_stage("w4_1%d" % a, 2 + a, w4_raw[a], -1.0) for a in range(2)]
+        w3q = order_w3(1)
+        for t in range(PACK):
+            activate(pages[0][t], 0, t, slice(0, T2 // CHUNK))
+
+        for pair in range(2):
+            for t in (2 * pair, 2 * pair + 1):
+                drive(w1q, damp1[t], t, stream[2 + t % 2][:])
+            for t in (2 * pair, 2 * pair + 1):
+                put_drive(pages[1][t], stream[2 + t % 2][:], t)
+
+        z0 = []
+        for mh in range(2):
+            grouped = grouped_ring[mh]
+            for c in range(2):
+                dst, src = weave_views(grouped[:, PACK * CHUNK * c : PACK * CHUNK * (c + 1)], 2 * mh + c)
+                nc.scalar.copy(dst, src)
+            z0.append(quantize("z0%d" % mh, grouped[:]))
+        woq = []
+        for b in range(HALVES):
+            grouped = grouped_ring[2 + b]
+            nc.scalar.copy(
+                grouped[:].rearrange("p (c i t) -> p c t i", i=4, t=PACK),
+                wo_raw[b][:].rearrange("p t (c i) -> p c t i", i=4),
+            )
+            woq.append(quantize("wo%d" % b, grouped[:]))
+
+        for t in range(PACK):
+            exchange(w3q, w4q, t)
+        for t in range(PACK):
+            put_exchange(pages[1][t], t)
+
+        accs = {}
+        for mh in range(2):
+            for n in range(PACK):
+                accs[mh, n] = bank(4 * (1 - mh) + n)
+                mm(accs[mh, n][:], woq[0][0][:, col128[n]].bitcast(FP8X4), woq[0][1][:, col128[n]],
+                   z0[mh][0].bitcast(FP8X4), z0[mh][1], True, False)
+
+        for t in range(PACK - 1):
+            activate(pages[1][t], 1, t, slice(0, T2 // CHUNK))
+        for mh in range(2):
+            codes = sb("z1_codes%d" % mh, [P, PASS], U32)
+            scales = sb("z1_scales%d" % mh, [P, PASS], U8)
+            for c in range(PASS // CHUNK):
+                part = slice(CHUNK * c, CHUNK * (c + 1))
+                chunk = 2 * mh + c
+                activate(pages[1][PACK - 1], 1, PACK - 1, slice(chunk, chunk + 1))
+                grouped = grouped_ring[chunk][:, 0 : PACK * CHUNK]
+                dst, src = weave_views(grouped, chunk)
+                nc.vector.tensor_copy(dst, src)
+                quantize(None, grouped, codes[:, part], scales[:, part])
+                for n in range(PACK):
+                    mm(accs[mh, n][:, part], woq[1][0][:, col128[n]].bitcast(FP8X4), woq[1][1][:, col128[n]],
+                       codes[:, part].bitcast(FP8X4), scales[:, part], False, part.stop == PASS)
+        for mh in range(2):
+            result = sb("result%d" % mh, [P, PACK, PASS], F32, tag="table%d" % mh)
+            for n in range(PACK):
+                if n % 2 == 1:
+                    nc.vector.tensor_copy(result[:, n, :], accs[mh, n][:])
+                else:
+                    nc.scalar.copy(result[:, n, :], accs[mh, n][:])
+                nc.sync.dma_start(out[col128[n], half_cols[mh]], result[:, n, :])

@@ -98,8 +98,8 @@ def tile_list_tokamak_edge_weave_kernel(
 
         def first_stage_views(slot, raw):
             grouped = grouped_ring[slot]
-            dst = grouped[:].rearrange("p (t m j) -> p m j t", t=PACK, j=PACK)
-            src = raw[:].rearrange("p j (m t) -> p m j t", t=PACK)
+            dst = grouped[:].rearrange("p (t m j) -> p m t j", t=PACK, j=PACK)
+            src = raw[:].rearrange("p j (m t) -> p m t j", t=PACK)
             return grouped, dst, src
 
         def mm(acc, lhs, lhs_s, rhs, rhs_s, start, stop):
@@ -163,7 +163,7 @@ def tile_list_tokamak_edge_weave_kernel(
         gain_sb = sb("gain_sb", [P, HALVES, PACK], F32)
         nc.sync.dma_start(gain_sb[:], gain.rearrange("(b p t) -> p b t", b=HALVES, t=PACK))
 
-        root = sb("root", [P, PACK, PACK, P], F32)
+        roots = [sb("root%d" % b, [P, PACK, PACK, P], F32) for b in range(HALVES)]
 
         def shear(b):
             for a in range(2):
@@ -172,17 +172,17 @@ def tile_list_tokamak_edge_weave_kernel(
                        w2c[b][:, a, :].bitcast(FP4X4),
                        w2_sc[:, H * a + PASS * b : H * a + PASS * (b + 1)], a == 0, a == 1)
 
-        def square_shear(ts):
+        def square_shear(b, ts):
             for c in range(PACK):
                 nc.scalar.activation(
-                    root[:, ts, c, :], bank(c)[:].rearrange("p (m t) -> p t m", t=PACK)[:, ts, :], ACT.Square
+                    roots[b][:, ts, c, :], bank(c)[:].rearrange("p (m t) -> p t m", t=PACK)[:, ts, :], ACT.Square
                 )
 
         def damping(b, t, turned):
-            flat = root[:, t, :, :]
+            flat = roots[b][:, t, :, :]
             nc.scalar.activation(flat, flat, ACT.Abs_reciprocal_sqrt, bias=1.0)
             for c in range(PACK):
-                nc.tensor.transpose(turned[:, col128[c]], root[:, t, c, :], ident[:])
+                nc.tensor.transpose(turned[:, col128[c]], roots[b][:, t, c, :], ident[:])
             damp = damp_ring[(PACK * b + t) % 6]
             nc.scalar.activation(damp[:], turned[:], ACT.Square)
             return damp
@@ -204,9 +204,9 @@ def tile_list_tokamak_edge_weave_kernel(
 
         pages = [[page_ring[(PACK * b + t) % 6] for t in range(PACK)] for b in range(HALVES)]
         shear(0)
-        square_shear(slice(0, 1))
+        square_shear(0, slice(0, 1))
         damp0 = [damping(0, 0, bank(7))]
-        square_shear(slice(1, PACK))
+        square_shear(0, slice(1, PACK))
 
         grouped, dst, src = first_stage_views(0, w1_raw0)
         nc.vector.tensor_copy(dst, src)
@@ -214,8 +214,8 @@ def tile_list_tokamak_edge_weave_kernel(
         grouped = grouped_ring[1]
         for h in range(2):
             nc.vector.tensor_copy(
-                grouped[:].rearrange("p (t m j) -> p m j t", t=PACK, j=PACK)[:, P // 2 * h : P // 2 * (h + 1), :, :],
-                w1_late[h][:].rearrange("p j (m t) -> p m j t", t=PACK),
+                grouped[:].rearrange("p (t m j) -> p m t j", t=PACK, j=PACK)[:, P // 2 * h : P // 2 * (h + 1), :, :],
+                w1_late[h][:].rearrange("p j (m t) -> p m t j", t=PACK),
             )
         codes = sb("w1_01_codes", [P, PASS], U32)
         scales = sb("w1_01_scales", [P, PASS], U8)
@@ -224,12 +224,13 @@ def tile_list_tokamak_edge_weave_kernel(
         w1q.append((codes[:], scales[:]))
         for t in range(PACK - 1):
             drive(w1q, damp0[t], t, stream[t % 2][:])
-            damp0.append(damping(0, t + 1, bank(4 + t)))
+            if t == 0:
+                damp0.extend([damping(0, later, bank(4)) for later in range(1, PACK)])
             put_drive(pages[0][t], stream[t % 2][:], t)
 
         load_w2(1, "w1_late0")
         shear(1)
-        square_shear(slice(0, PACK))
+        square_shear(1, slice(0, PACK))
 
         v2_sc = gather("v2_sc", tab2_sc[:], idx2, U8)
         v2 = [gather("v2_%d" % a, tab2[a][:], idx2, U32) for a in range(2)]
@@ -242,8 +243,8 @@ def tile_list_tokamak_edge_weave_kernel(
             )
             scales = sb("w3s%d" % b, [P, PASS], U8)
             nc.vector.tensor_copy(
-                scales[:].rearrange("p (t m) -> p m t", t=PACK),
-                w3_sc[:, half_cols[b]].rearrange("p (m t) -> p m t", t=PACK),
+                scales[:].rearrange("p (t m) -> p t m", t=PACK),
+                w3_sc[:, half_cols[b]].rearrange("p (m t) -> p t m", t=PACK),
             )
             return codes, scales
 
@@ -263,9 +264,9 @@ def tile_list_tokamak_edge_weave_kernel(
         z_pairs = sb("z_pairs", [P, PACK * T2], BF16)
         z_slots = z_pairs[:].rearrange("p (c u m e) -> p u e c m", u=2, e=2, m=CHUNK)
         z_words = z_pairs[:].bitcast(F32)
-        th = sb("th", [P, T2], F32)
+        ths = [sb("th0", [P, T2], F32), sb("th1", [P, T2], F32, tag="w1_late1")]
 
-        def activate(page, b, t, chunks):
+        def activate(page, b, t, chunks, th):
             cols = slice(CHUNK * chunks.start, CHUNK * chunks.stop)
             nc.scalar.activation(th[:, cols], page[:, cols], ACT.Tanh)
             nc.scalar.activation(
@@ -274,8 +275,8 @@ def tile_list_tokamak_edge_weave_kernel(
             )
 
         def weave_views(grouped, chunk):
-            dst = grouped.bitcast(F32).rearrange("p (c i u) -> p c u i", i=4, u=2)
-            src = z_words[:, 2 * CHUNK * chunk : 2 * CHUNK * (chunk + 1)].rearrange("p (u c i) -> p c u i", i=4, u=2)
+            dst = grouped.bitcast(F32).rearrange("p (m u) -> p m u", u=2)
+            src = z_words[:, 2 * CHUNK * chunk : 2 * CHUNK * (chunk + 1)].rearrange("p (u m) -> p m u", u=2)
             return dst, src
 
         w3q = order_w3(0)
@@ -287,23 +288,23 @@ def tile_list_tokamak_edge_weave_kernel(
 
         w1_raw = [load_rows(a, w1, a, half_cols[1]) for a in range(2)]
         w4_raw = [load_rows(2 + a, w4, a, half_cols[1]) for a in range(2)]
-        w1q = [cast_first_stage("w1_1%d" % a, a, w1_raw[a], 1.0) for a in range(2)]
-        wo_raw = [load_rows(b, wo, b, slice(0, N)) for b in range(HALVES)]
-
         for t in range(PACK):
             exchange(w3q, w4q, t)
+        w1q = [cast_first_stage("w1_1%d" % a, a, w1_raw[a], 1.0) for a in range(2)]
+        wo_raw = [load_rows(b, wo, b, slice(0, N)) for b in range(HALVES)]
         for t in range(PACK):
             put_exchange(pages[0][t], t)
         w4q = [cast_first_stage("w4_1%d" % a, 2 + a, w4_raw[a], -1.0) for a in range(2)]
         w3q = order_w3(1)
         for t in range(PACK):
-            activate(pages[0][t], 0, t, slice(0, T2 // CHUNK))
+            activate(pages[0][t], 0, t, slice(0, T2 // CHUNK), ths[t % 2])
 
+        h1 = [grouped_ring[3 - i][:, 0 : 2 * S].bitcast(F32) for i in range(2)]
         for pair in range(2):
             for t in (2 * pair, 2 * pair + 1):
-                drive(w1q, damp1[t], t, stream[2 + t % 2][:])
+                drive(w1q, damp1[t], t, h1[t % 2])
             for t in (2 * pair, 2 * pair + 1):
-                put_drive(pages[1][t], stream[2 + t % 2][:], t)
+                put_drive(pages[1][t], h1[t % 2], t)
 
         z0 = []
         for mh in range(2):
@@ -313,13 +314,14 @@ def tile_list_tokamak_edge_weave_kernel(
                 nc.scalar.copy(dst, src)
             z0.append(quantize("z0%d" % mh, grouped[:]))
         woq = []
+        wo_grouped = sb("wo_grouped", [P, HALVES * PACK * N], BF16, tag="w3_raw")
         for b in range(HALVES):
-            grouped = grouped_ring[2 + b]
+            grouped = wo_grouped[:, PACK * N * b : PACK * N * (b + 1)]
             nc.scalar.copy(
-                grouped[:].rearrange("p (c i t) -> p c t i", i=4, t=PACK),
-                wo_raw[b][:].rearrange("p t (c i) -> p c t i", i=4),
+                grouped.rearrange("p (n t) -> p n t", t=PACK),
+                wo_raw[b][:].rearrange("p t n -> p n t"),
             )
-            woq.append(quantize("wo%d" % b, grouped[:]))
+            woq.append(quantize("wo%d" % b, grouped))
 
         for t in range(PACK):
             exchange(w3q, w4q, t)
@@ -334,14 +336,14 @@ def tile_list_tokamak_edge_weave_kernel(
                    z0[mh][0].bitcast(FP8X4), z0[mh][1], True, False)
 
         for t in range(PACK - 1):
-            activate(pages[1][t], 1, t, slice(0, T2 // CHUNK))
+            activate(pages[1][t], 1, t, slice(0, T2 // CHUNK), ths[0])
         for mh in range(2):
             codes = sb("z1_codes%d" % mh, [P, PASS], U32)
             scales = sb("z1_scales%d" % mh, [P, PASS], U8)
             for c in range(PASS // CHUNK):
                 part = slice(CHUNK * c, CHUNK * (c + 1))
                 chunk = 2 * mh + c
-                activate(pages[1][PACK - 1], 1, PACK - 1, slice(chunk, chunk + 1))
+                activate(pages[1][PACK - 1], 1, PACK - 1, slice(chunk, chunk + 1), ths[0])
                 grouped = grouped_ring[chunk][:, 0 : PACK * CHUNK]
                 dst, src = weave_views(grouped, chunk)
                 nc.vector.tensor_copy(dst, src)

@@ -23,6 +23,7 @@ PASS = P * PACK
 QUADS = 4
 HALVES = 2
 CHUNK = 256
+RUN = 4
 
 
 def tile_list_tokamak_edge_weave_kernel(
@@ -78,11 +79,11 @@ def tile_list_tokamak_edge_weave_kernel(
             nc.sync.dma_start(raw[:], w[PASS * a : PASS * (a + 1), cols].rearrange("(p j) c -> p j c", j=PACK))
             return raw
 
-        def load_cell_weights(name, wg):
-            tile = sb(name, [P, PACK, S], F32)
+        def load_cell_weights(tile, wg, t):
             for q in range(QUADS):
-                nc.sync.dma_start(tile[32 * q : 32 * (q + 1), :, :], wg.rearrange("(q t) j -> q t j", t=PACK))
-            return tile
+                nc.sync.dma_start(
+                    tile[32 * q : 32 * (q + 1), t, :], wg.rearrange("(y t x) j -> t y x j", t=PACK, x=RUN)[t]
+                )
 
         def gather(name, window, offsets, dtype):
             picked = sb(name, [P, S], dtype)
@@ -98,8 +99,8 @@ def tile_list_tokamak_edge_weave_kernel(
 
         def first_stage_views(slot, raw):
             grouped = grouped_ring[slot]
-            dst = grouped[:].rearrange("p (t m j) -> p m t j", t=PACK, j=PACK)
-            src = raw[:].rearrange("p j (m t) -> p m t j", t=PACK)
+            dst = grouped[:].rearrange("p (t y x j) -> p t y x j", t=PACK, x=RUN, j=PACK)
+            src = raw[:].rearrange("p j (y t x) -> p t y x j", t=PACK, x=RUN)
             return grouped, dst, src
 
         def mm(acc, lhs, lhs_s, rhs, rhs_s, start, stop):
@@ -144,7 +145,13 @@ def tile_list_tokamak_edge_weave_kernel(
             )
             w1_late.append(piece)
         idx3 = load_list("idx3", offs3)
-        wg1_sb = load_cell_weights("wg1_sb", wg1)
+        wg1_sb = sb("wg1_sb", [P, PACK, S], F32)
+        load_cell_weights(wg1_sb, wg1, 0)
+        load_w2(1, "w1_late0")
+        w4_raw = []
+        for a in range(2):
+            load_cell_weights(wg1_sb, wg1, 1 + a)
+            w4_raw.append(load_rows(2 + a, w4, a, half_cols[0]))
 
         v, v_sc = [], []
         for a in range(2):
@@ -157,11 +164,9 @@ def tile_list_tokamak_edge_weave_kernel(
         load_scales_stacked(w3_sc, w3_scales)
         w3_raw = sb("w3_raw", [P, 2, H], I32)
         nc.sync.dma_start(w3_raw[:], w3_words.rearrange("a p c i -> p a (c i)").bitcast(I32))
-        w4_raw = [load_rows(2 + a, w4, a, half_cols[0]) for a in range(2)]
+        load_cell_weights(wg1_sb, wg1, PACK - 1)
         idx4 = load_list("idx4", offs4)
-        wg2_sb = load_cell_weights("wg2_sb", wg2)
-        gain_sb = sb("gain_sb", [P, HALVES, PACK], F32)
-        nc.sync.dma_start(gain_sb[:], gain.rearrange("(b p t) -> p b t", b=HALVES, t=PACK))
+        wg2_sb = sb("wg2_sb", [P, PACK, S], F32)
 
         roots = [sb("root%d" % b, [P, PACK, PACK, P], F32) for b in range(HALVES)]
 
@@ -175,14 +180,16 @@ def tile_list_tokamak_edge_weave_kernel(
         def square_shear(b, ts):
             for c in range(PACK):
                 nc.scalar.activation(
-                    roots[b][:, ts, c, :], bank(c)[:].rearrange("p (m t) -> p t m", t=PACK)[:, ts, :], ACT.Square
+                    roots[b][:, ts, c, :].rearrange("p t (y x) -> p t y x", x=RUN),
+                    bank(c)[:].rearrange("p (y t x) -> p t y x", t=PACK, x=RUN)[:, ts, :, :],
+                    ACT.Square,
                 )
 
-        def damping(b, t, turned):
-            flat = roots[b][:, t, :, :]
-            nc.scalar.activation(flat, flat, ACT.Abs_reciprocal_sqrt, bias=1.0)
+        def damping(b, t, root, turned):
+            squares = roots[b][:, t, :, :].rearrange("p c m -> p (c m)")
+            nc.scalar.activation(root, squares, ACT.Abs_reciprocal_sqrt, bias=1.0)
             for c in range(PACK):
-                nc.tensor.transpose(turned[:, col128[c]], roots[b][:, t, c, :], ident[:])
+                nc.tensor.transpose(turned[:, col128[c]], root[:, col128[c]], ident[:])
             damp = damp_ring[(PACK * b + t) % 6]
             nc.scalar.activation(damp[:], turned[:], ACT.Square)
             return damp
@@ -199,13 +206,18 @@ def tile_list_tokamak_edge_weave_kernel(
 
         def cast_first_stage(name, slot, raw, scale):
             grouped, dst, src = first_stage_views(slot, raw)
-            nc.scalar.activation(dst, src, ACT.Copy, scale=scale)
+            if scale == 1.0:
+                nc.scalar.copy(dst, src)
+            else:
+                for t in range(PACK):
+                    nc.scalar.activation(dst[:, t, :, :, :], src[:, t, :, :, :], ACT.Copy, scale=scale)
             return quantize(name, grouped[:])
 
         pages = [[page_ring[(PACK * b + t) % 6] for t in range(PACK)] for b in range(HALVES)]
         shear(0)
         square_shear(0, slice(0, 1))
-        damp0 = [damping(0, 0, bank(7))]
+        in_place = [roots[0][:, t, :, :].rearrange("p c m -> p (c m)") for t in range(PACK)]
+        damp0 = [damping(0, 0, in_place[0], bank(7))]
         square_shear(0, slice(1, PACK))
 
         grouped, dst, src = first_stage_views(0, w1_raw0)
@@ -214,8 +226,8 @@ def tile_list_tokamak_edge_weave_kernel(
         grouped = grouped_ring[1]
         for h in range(2):
             nc.vector.tensor_copy(
-                grouped[:].rearrange("p (t m j) -> p m t j", t=PACK, j=PACK)[:, P // 2 * h : P // 2 * (h + 1), :, :],
-                w1_late[h][:].rearrange("p j (m t) -> p m t j", t=PACK),
+                grouped[:].rearrange("p (t y x j) -> p t y x j", t=PACK, x=RUN, j=PACK)[:, :, 16 * h : 16 * (h + 1), :, :],
+                w1_late[h][:].rearrange("p j (y t x) -> p t y x j", t=PACK, x=RUN),
             )
         codes = sb("w1_01_codes", [P, PASS], U32)
         scales = sb("w1_01_scales", [P, PASS], U8)
@@ -225,33 +237,31 @@ def tile_list_tokamak_edge_weave_kernel(
         for t in range(PACK - 1):
             drive(w1q, damp0[t], t, stream[t % 2][:])
             if t == 0:
-                damp0.extend([damping(0, later, bank(4)) for later in range(1, PACK)])
+                damp0.extend([damping(0, later, in_place[later], bank(4)) for later in range(1, PACK)])
             put_drive(pages[0][t], stream[t % 2][:], t)
 
-        load_w2(1, "w1_late0")
         shear(1)
         square_shear(1, slice(0, PACK))
 
         v2_sc = gather("v2_sc", tab2_sc[:], idx2, U8)
         v2 = [gather("v2_%d" % a, tab2[a][:], idx2, U32) for a in range(2)]
 
-        def order_w3(b):
-            codes = sb("w3c%d" % b, [P, 2, PASS], I32)
-            nc.vector.tensor_copy(
-                codes[:].rearrange("p a (t m) -> p a m t", t=PACK),
-                w3_raw[:, :, half_cols[b]].rearrange("p a (m t) -> p a m t", t=PACK),
-            )
-            scales = sb("w3s%d" % b, [P, PASS], U8)
-            nc.vector.tensor_copy(
-                scales[:].rearrange("p (t m) -> p t m", t=PACK),
-                w3_sc[:, half_cols[b]].rearrange("p (m t) -> p t m", t=PACK),
-            )
-            return codes, scales
+        w3s = sb("w3s", [P, H], U8)
+        nc.vector.tensor_copy(
+            w3s[:].bitcast(I32).rearrange("p (b t y) -> p b t y", b=HALVES, t=PACK),
+            w3_sc[:].bitcast(I32).rearrange("p (b y t) -> p b t y", b=HALVES, t=PACK),
+        )
+        w3c = sb("w3c", [P, 2 * H], I32)
+        nc.vector.tensor_copy(
+            w3c[:].rearrange("p (g t y x) -> p g t y x", g=2 * HALVES, t=PACK, x=RUN),
+            w3_raw[:].rearrange("p a (b y t x) -> p (a b) t y x", b=HALVES, t=PACK, x=RUN),
+        )
 
-        def exchange(w3q, w4q, t):
+        def exchange(b, w4q, t):
             acc = bank(t)
             for a in range(2):
-                mm(acc[:], w3q[0][:, a, col128[t]].bitcast(FP8X4), w3q[1][4 * a : P, col128[t]],
+                lo = PASS * b + P * t
+                mm(acc[:], w3c[:, H * a + lo : H * a + lo + P].bitcast(FP8X4), w3s[4 * a : P, lo : lo + P],
                    v2[a][:].bitcast(FP8X4), v2_sc[4 * a : P, :], a == 0, False)
             for a in range(2):
                 mm(acc[:], w4q[a][0][:, col128[t]].bitcast(FP8X4), w4q[a][1][:, col128[t]],
@@ -261,45 +271,54 @@ def tile_list_tokamak_edge_weave_kernel(
         def put_exchange(page, t):
             nc.vector.tensor_tensor(page[:].indirect(idx4[:]), stream[t][:], wg2_sb[:, t, :], MULT)
 
-        z_pairs = sb("z_pairs", [P, PACK * T2], BF16)
-        z_slots = z_pairs[:].rearrange("p (c u m e) -> p u e c m", u=2, e=2, m=CHUNK)
-        z_words = z_pairs[:].bitcast(F32)
-        ths = [sb("th0", [P, T2], F32), sb("th1", [P, T2], F32, tag="w1_late1")]
+        z_rows = sb("z_rows", [P, PACK * T2], BF16)[:].rearrange("p (c t m) -> p c t m", t=PACK, m=CHUNK)
+        ths = [raw_ring[3][:, 2 * i : 2 * i + 2, :].rearrange("p j c -> p (j c)") for i in range(2)]
 
         def activate(page, b, t, chunks, th):
             cols = slice(CHUNK * chunks.start, CHUNK * chunks.stop)
             nc.scalar.activation(th[:, cols], page[:, cols], ACT.Tanh)
             nc.scalar.activation(
-                z_slots[:, t // 2, t % 2, chunks, :], th[:, cols].rearrange("p (c m) -> p c m", m=CHUNK),
-                ACT.Copy, scale=gain_sb[:, b, t : t + 1],
+                z_rows[:, chunks, t, :], th[:, cols].rearrange("p (c m) -> p c m", m=CHUNK),
+                ACT.Copy, scale=gain_sb[:, b, t, 0:1],
             )
 
         def weave_views(grouped, chunk):
-            dst = grouped.bitcast(F32).rearrange("p (m u) -> p m u", u=2)
-            src = z_words[:, 2 * CHUNK * chunk : 2 * CHUNK * (chunk + 1)].rearrange("p (u m) -> p m u", u=2)
-            return dst, src
+            return grouped.rearrange("p (m t) -> p m t", t=PACK), z_rows[:, chunk, :, :].rearrange("p t m -> p m t")
 
-        w3q = order_w3(0)
         w4q = [cast_first_stage("w4_0%d" % a, 2 + a, w4_raw[a], -1.0) for a in range(2)]
-        damp1 = [damping(1, t, bank(t)) for t in range(PACK)]
-        held = grouped_ring[3][:, 0 : 2 * S].bitcast(F32)
+        damp1 = [damping(1, t, raw_ring[3][:, t, :], bank(4 + t % 3)) for t in range(PACK)]
+        held = sb("held", [P, S], F32, tag="w3_raw")[:]
         drive(w1q, damp0[PACK - 1], PACK - 1, held)
         put_drive(pages[0][PACK - 1], held, PACK - 1)
 
-        w1_raw = [load_rows(a, w1, a, half_cols[1]) for a in range(2)]
-        w4_raw = [load_rows(2 + a, w4, a, half_cols[1]) for a in range(2)]
+        gain_sb = sb("gain_sb", [P, HALVES, PACK, 8], F32)
+        gain_rows = gain.rearrange("(b y t x o) -> b t y x o", b=HALVES, t=PACK, x=RUN, o=1)
+        second = []
+        for t, w in enumerate((w1, w1, w4, w4)):
+            load_cell_weights(wg2_sb, wg2, t)
+            second.append(load_rows(t, w, t % 2, half_cols[1]))
+        with nc.allow_non_contiguous_dma(reason="one gain value for each partition"):
+            for b in range(HALVES):
+                for t in range(PACK):
+                    nc.sync.dma_start(gain_sb[:, b, t, 0:1], gain_rows[b, t])
+        w1_raw, w4_raw = second[:2], second[2:]
         for t in range(PACK):
-            exchange(w3q, w4q, t)
+            exchange(0, w4q, t)
         w1q = [cast_first_stage("w1_1%d" % a, a, w1_raw[a], 1.0) for a in range(2)]
-        wo_raw = [load_rows(b, wo, b, slice(0, N)) for b in range(HALVES)]
+        wo_raw = raw_ring[0:HALVES]
+        for b in range(HALVES):
+            for t in range(PACK):
+                nc.sync.dma_start(
+                    wo_raw[b][:, t, :],
+                    wo[PASS * b : PASS * (b + 1), :].rearrange("(y t x) n -> t y x n", t=PACK, x=RUN)[t],
+                )
         for t in range(PACK):
             put_exchange(pages[0][t], t)
         w4q = [cast_first_stage("w4_1%d" % a, 2 + a, w4_raw[a], -1.0) for a in range(2)]
-        w3q = order_w3(1)
         for t in range(PACK):
             activate(pages[0][t], 0, t, slice(0, T2 // CHUNK), ths[t % 2])
 
-        h1 = [grouped_ring[3 - i][:, 0 : 2 * S].bitcast(F32) for i in range(2)]
+        h1 = [grouped_ring[3][:, 2 * S * i : 2 * S * (i + 1)].bitcast(F32) for i in range(2)]
         for pair in range(2):
             for t in (2 * pair, 2 * pair + 1):
                 drive(w1q, damp1[t], t, h1[t % 2])
@@ -312,7 +331,10 @@ def tile_list_tokamak_edge_weave_kernel(
             for c in range(2):
                 dst, src = weave_views(grouped[:, PACK * CHUNK * c : PACK * CHUNK * (c + 1)], 2 * mh + c)
                 nc.scalar.copy(dst, src)
-            z0.append(quantize("z0%d" % mh, grouped[:]))
+            if mh == 0:
+                z0.append(quantize("z00", grouped[:]))
+        for t in range(PACK - 1):
+            exchange(1, w4q, t)
         woq = []
         wo_grouped = sb("wo_grouped", [P, HALVES * PACK * N], BF16, tag="w3_raw")
         for b in range(HALVES):
@@ -321,13 +343,17 @@ def tile_list_tokamak_edge_weave_kernel(
                 grouped.rearrange("p (n t) -> p n t", t=PACK),
                 wo_raw[b][:].rearrange("p t n -> p n t"),
             )
-            woq.append(quantize("wo%d" % b, grouped))
+            if b == 0:
+                woq.append(quantize("wo0", grouped))
 
-        for t in range(PACK):
-            exchange(w3q, w4q, t)
+        exchange(1, w4q, PACK - 1)
         for t in range(PACK):
             put_exchange(pages[1][t], t)
 
+        late_codes = sb("late_codes", [P, 2 * PASS], U32, tag="wg2_sb")
+        late_scales = sb("late_scales", [P, 2 * PASS], U8)
+        z0.append(quantize(None, grouped_ring[1][:], late_codes[:, half_cols[0]], late_scales[:, half_cols[0]]))
+        woq.append(quantize(None, wo_grouped[:, PACK * N :], late_codes[:, half_cols[1]], late_scales[:, half_cols[1]]))
         accs = {}
         for mh in range(2):
             for n in range(PACK):
@@ -338,19 +364,16 @@ def tile_list_tokamak_edge_weave_kernel(
         for t in range(PACK - 1):
             activate(pages[1][t], 1, t, slice(0, T2 // CHUNK), ths[0])
         for mh in range(2):
-            codes = sb("z1_codes%d" % mh, [P, PASS], U32)
-            scales = sb("z1_scales%d" % mh, [P, PASS], U8)
+            grouped = grouped_ring[2]
             for c in range(PASS // CHUNK):
-                part = slice(CHUNK * c, CHUNK * (c + 1))
                 chunk = 2 * mh + c
                 activate(pages[1][PACK - 1], 1, PACK - 1, slice(chunk, chunk + 1), ths[0])
-                grouped = grouped_ring[chunk][:, 0 : PACK * CHUNK]
-                dst, src = weave_views(grouped, chunk)
+                dst, src = weave_views(grouped[:, PACK * CHUNK * c : PACK * CHUNK * (c + 1)], chunk)
                 nc.vector.tensor_copy(dst, src)
-                quantize(None, grouped, codes[:, part], scales[:, part])
-                for n in range(PACK):
-                    mm(accs[mh, n][:, part], woq[1][0][:, col128[n]].bitcast(FP8X4), woq[1][1][:, col128[n]],
-                       codes[:, part].bitcast(FP8X4), scales[:, part], False, part.stop == PASS)
+            codes, scales = quantize("z1%d" % mh, grouped[:])
+            for n in range(PACK):
+                mm(accs[mh, n][:], woq[1][0][:, col128[n]].bitcast(FP8X4), woq[1][1][:, col128[n]],
+                   codes.bitcast(FP8X4), scales, False, True)
         for mh in range(2):
             result = sb("result%d" % mh, [P, PACK, PASS], F32, tag="table%d" % mh)
             for n in range(PACK):

@@ -99,8 +99,8 @@ def tile_list_tokamak_edge_weave_kernel(
 
         def first_stage_views(slot, raw):
             grouped = grouped_ring[slot]
-            dst = grouped[:].rearrange("p (t y x j) -> p t y x j", t=PACK, x=RUN, j=PACK)
-            src = raw[:].rearrange("p j (y t x) -> p t y x j", t=PACK, x=RUN)
+            dst = grouped[:].rearrange("p (t y x j) -> p t y j x", t=PACK, x=RUN, j=PACK)
+            src = raw[:].rearrange("p j (y t x) -> p t y j x", t=PACK, x=RUN)
             return grouped, dst, src
 
         def mm(acc, lhs, lhs_s, rhs, rhs_s, start, stop):
@@ -226,8 +226,8 @@ def tile_list_tokamak_edge_weave_kernel(
         grouped = grouped_ring[1]
         for h in range(2):
             nc.vector.tensor_copy(
-                grouped[:].rearrange("p (t y x j) -> p t y x j", t=PACK, x=RUN, j=PACK)[:, :, 16 * h : 16 * (h + 1), :, :],
-                w1_late[h][:].rearrange("p j (y t x) -> p t y x j", t=PACK, x=RUN),
+                grouped[:].rearrange("p (t y x j) -> p t y j x", t=PACK, x=RUN, j=PACK)[:, :, 16 * h : 16 * (h + 1), :, :],
+                w1_late[h][:].rearrange("p j (y t x) -> p t y j x", t=PACK, x=RUN),
             )
         codes = sb("w1_01_codes", [P, PASS], U32)
         scales = sb("w1_01_scales", [P, PASS], U8)
@@ -283,7 +283,10 @@ def tile_list_tokamak_edge_weave_kernel(
             )
 
         def weave_views(grouped, chunk):
-            return grouped.rearrange("p (m t) -> p m t", t=PACK), z_rows[:, chunk, :, :].rearrange("p t m -> p m t")
+            return (
+                grouped.rearrange("p (c i t) -> p c t i", t=PACK, i=RUN),
+                z_rows[:, chunk, :, :].rearrange("p t (c i) -> p c t i", i=RUN),
+            )
 
         w4q = [cast_first_stage("w4_0%d" % a, 2 + a, w4_raw[a], -1.0) for a in range(2)]
         damp1 = [damping(1, t, raw_ring[3][:, t, :], bank(4 + t % 3)) for t in range(PACK)]
@@ -295,8 +298,8 @@ def tile_list_tokamak_edge_weave_kernel(
         gain_rows = gain.rearrange("(b y t x o) -> b t y x o", b=HALVES, t=PACK, x=RUN, o=1)
         second = []
         for t, w in enumerate((w1, w1, w4, w4)):
-            load_cell_weights(wg2_sb, wg2, t)
             second.append(load_rows(t, w, t % 2, half_cols[1]))
+            load_cell_weights(wg2_sb, wg2, t)
         with nc.allow_non_contiguous_dma(reason="one gain value for each partition"):
             for b in range(HALVES):
                 for t in range(PACK):
@@ -340,8 +343,8 @@ def tile_list_tokamak_edge_weave_kernel(
         for b in range(HALVES):
             grouped = wo_grouped[:, PACK * N * b : PACK * N * (b + 1)]
             nc.scalar.copy(
-                grouped.rearrange("p (n t) -> p n t", t=PACK),
-                wo_raw[b][:].rearrange("p t n -> p n t"),
+                grouped.rearrange("p (c i t) -> p c t i", t=PACK, i=RUN),
+                wo_raw[b][:].rearrange("p t (c i) -> p c t i", i=RUN),
             )
             if b == 0:
                 woq.append(quantize("wo0", grouped))
@@ -377,7 +380,7 @@ def tile_list_tokamak_edge_weave_kernel(
         for mh in range(2):
             result = sb("result%d" % mh, [P, PACK, PASS], F32, tag="table%d" % mh)
             for n in range(PACK):
-                if n % 2 == 1:
+                if mh == 1 and n % 2 == 1:
                     nc.vector.tensor_copy(result[:, n, :], accs[mh, n][:])
                 else:
                     nc.scalar.copy(result[:, n, :], accs[mh, n][:])

@@ -20,10 +20,15 @@ MULT = mybir.AluOpType.mult
 P = 128
 PACK = 4
 PASS = P * PACK
-QUADS = 4
-HALVES = 2
-CHUNK = 256
+PASSES = K // PASS
+HALVES = H // PASS
 RUN = 4
+CHUNK = 256
+LAST = PACK - 1
+QUADRANTS = (0, 2, 1, 3)
+STAGES = 4
+RINGS = 6
+GAIN_PITCH = 8
 
 
 def tile_list_tokamak_edge_weave_kernel(
@@ -36,23 +41,23 @@ def tile_list_tokamak_edge_weave_kernel(
         keep = ctx.enter_context(tc.tile_pool(name="keep", bufs=1))
         psum = ctx.enter_context(tc.psum_pool(name="psum", bufs=1))
 
-        def sb(name, shape, dtype, tag=None, bufs=1):
-            return keep.tile(shape, dtype, name=name, tag=tag or name, bufs=bufs, align_bytes=64)
+        def sb(name, shape, dtype, tag=None):
+            return keep.tile(shape, dtype, name=name, tag=tag or name, align_bytes=64)
 
-        banks = [psum.tile([P, PASS], F32, name="bank%d" % b) for b in range(8)]
+        banks = [psum.tile([P, PASS], F32, name="bank%d" % i) for i in range(8)]
+        raw = [sb("raw%d" % i, [P, PACK, PASS], F32) for i in range(STAGES)]
+        grouped = [sb("grouped%d" % i, [P, PACK * PASS], BF16) for i in range(STAGES)]
+        stream = [sb("stream%d" % i, [P, S], F32) for i in range(PACK)]
+        damp_ring = [sb("damp%d" % i, [P, S], F32) for i in range(RINGS)]
+        page_ring = [sb("page%d" % i, [P, T2], F32) for i in range(RINGS)]
+        pages = [[page_ring[(PACK * b + t) % RINGS] for t in range(PACK)] for b in range(HALVES)]
 
-        def bank(b):
-            return banks[b]
+        cols512 = [slice(PASS * i, PASS * (i + 1)) for i in range(2)]
+        cols128 = [slice(P * i, P * (i + 1)) for i in range(PACK)]
 
-        raw_ring = [sb("raw%d" % i, [P, PACK, PASS], F32) for i in range(4)]
-        grouped_ring = [sb("grouped%d" % i, [P, PACK * PASS], BF16) for i in range(4)]
-        stream = [sb("stream%d" % i, [P, S], F32) for i in range(4)]
-        damp_ring = [sb("damp%d" % i, [P, S], F32) for i in range(6)]
-        page_ring = [sb("page%d" % i, [P, T2], F32) for i in range(6)]
-
-        def load_list(name, src):
+        def load_list(name, offsets):
             tile = lists.tile([P, S // 16], U16, name=name)
-            nc.sync.dma_start(tile[:], src)
+            nc.sync.dma_start(tile[:], offsets)
             return tile
 
         def load_table_words(name, words, a):
@@ -60,328 +65,318 @@ def tile_list_tokamak_edge_weave_kernel(
             nc.sync.dma_start(tile[:].bitcast(I32), words[a].rearrange("p n i -> p (n i)").bitcast(I32))
             return tile
 
-        def load_scales_side_by_side(tile, scales):
-            for q in range(QUADS):
+        def load_planes_side_by_side(tile, scales):
+            for q in QUADRANTS:
                 nc.sync.dma_start(
-                    tile[32 * q : 32 * q + 4, :].bitcast(I32).rearrange("r (a n) -> r a n", a=2),
+                    tile[32 * q : 32 * q + 4, :].bitcast(I32).rearrange("r (a n) -> r a n", a=PASSES),
                     scales[:, 4 * q : 4 * q + 4, :].bitcast(I32).rearrange("a r n -> r a n"),
                 )
 
-        def load_scales_stacked(tile, scales):
-            for q in range(QUADS):
+        def load_planes_stacked(tile, scales):
+            for q in QUADRANTS:
                 nc.sync.dma_start(
                     tile[32 * q : 32 * q + 8, :].bitcast(I32),
                     scales[:, 4 * q : 4 * q + 4, :].bitcast(I32),
                 )
 
-        def load_rows(slot, w, a, cols):
-            raw = raw_ring[slot]
-            nc.sync.dma_start(raw[:], w[PASS * a : PASS * (a + 1), cols].rearrange("(p j) c -> p j c", j=PACK))
-            return raw
+        def load_k_rows(tile, w, a, cols):
+            nc.sync.dma_start(tile[:], w[cols512[a], cols].rearrange("(p j) c -> p j c", j=PACK))
 
         def load_cell_weights(tile, wg, t):
-            for q in range(QUADS):
+            for q in QUADRANTS:
                 nc.sync.dma_start(
                     tile[32 * q : 32 * (q + 1), t, :], wg.rearrange("(y t x) j -> t y x j", t=PACK, x=RUN)[t]
                 )
+
+        def load_w2(b, tag):
+            tile = sb("w2_codes%d" % b, [P, PASSES, 2 * PASS], U8, tag=tag)
+            nc.sync.dma_start(
+                tile[:].bitcast(I32),
+                w2_words[:, :, 2 * PASS * b : 2 * PASS * (b + 1)].bitcast(I32).rearrange("a p n -> p a n"),
+            )
+            return tile
 
         def gather(name, window, offsets, dtype):
             picked = sb(name, [P, S], dtype)
             nc.vector.tensor_copy(picked[:], window.indirect(offsets[:]))
             return picked
 
-        def quantize(name, grouped, codes=None, scales=None):
-            if codes is None:
-                codes = sb(name + "_codes", [P, PASS], U32)[:]
-                scales = sb(name + "_scales", [P, PASS], U8)[:]
-            nc.vector.quantize_mx(out=codes.bitcast(FP8X4), scales=scales, in_=grouped)
+        def quantize_into(codes, scales, values):
+            nc.vector.quantize_mx(out=codes.bitcast(FP8X4), scales=scales, in_=values)
             return codes, scales
 
-        def first_stage_views(slot, raw):
-            grouped = grouped_ring[slot]
-            dst = grouped[:].rearrange("p (t y x j) -> p t y j x", t=PACK, x=RUN, j=PACK)
-            src = raw[:].rearrange("p j (y t x) -> p t y j x", t=PACK, x=RUN)
-            return grouped, dst, src
+        def quantize(name, values, tag=None):
+            codes = sb(name + "_codes", [P, PASS], U32, tag=tag)
+            scales = sb(name + "_scales", [P, PASS], U8)
+            return quantize_into(codes[:], scales[:], values)
 
-        def mm(acc, lhs, lhs_s, rhs, rhs_s, start, stop):
-            nc.tensor.matmul_mx(out=acc, lhsT=lhs, lhsT_scale=lhs_s, rhs=rhs, rhs_scale=rhs_s, start=start, stop=stop)
+        def mm(acc, lhs, lhs_scale, rhs, rhs_scale, start, stop):
+            nc.tensor.matmul_mx(
+                out=acc, lhsT=lhs, lhsT_scale=lhs_scale, rhs=rhs, rhs_scale=rhs_scale, start=start, stop=stop
+            )
 
-        half_cols = [slice(PASS * b, PASS * (b + 1)) for b in range(HALVES)]
-        col128 = [slice(P * t, P * (t + 1)) for t in range(PACK)]
+        def mm_fp8(acc, lhs, cols, rhs, start, stop):
+            mm(acc[:], lhs[0][:, cols].bitcast(FP8X4), lhs[1][:, cols], rhs[0].bitcast(FP8X4), rhs[1], start, stop)
 
-        tab_sc = sb("tab_sc", [P, 2 * T], U8)
-        w2_sc = sb("w2_sc", [P, 2 * H], U8)
-        tab2_sc = sb("tab2_sc", [P, T], U8)
-        w3_sc = sb("w3_sc", [P, H], U8)
-        nc.vector.memset(tab_sc[:].bitcast(I32), 0)
-        nc.vector.memset(w2_sc[:].bitcast(I32), 0)
-        nc.vector.memset(tab2_sc[:].bitcast(I32), 0)
-        nc.vector.memset(w3_sc[:].bitcast(I32), 0)
+        def words_view(tile):
+            return tile[:].rearrange("p (t y x j) -> p t y j x", t=PACK, x=RUN, j=PACK)
+
+        def rows_view(tile):
+            return tile[:].rearrange("p j (y t x) -> p t y j x", t=PACK, x=RUN)
+
+        def quantize_negated_w4(b, a, tag=None):
+            stage = PASSES + a
+            for t in range(PACK):
+                nc.scalar.activation(
+                    words_view(grouped[stage])[:, t, :, :, :], rows_view(raw[stage])[:, t, :, :, :], ACT.Copy, scale=-1.0
+                )
+            return quantize("w4_%d%d" % (b, a), grouped[stage][:], tag=tag)
+
+        def interleave(engine_copy, words, rows):
+            engine_copy(
+                words.rearrange("p (c i t) -> p c t i", t=PACK, i=RUN), rows.rearrange("p t (c i) -> p c t i", i=RUN)
+            )
+
+        tab_planes = sb("tab_planes", [P, PASSES * T], U8)
+        w2_planes = sb("w2_planes", [P, PASSES * H], U8)
+        tab2_planes = sb("tab2_planes", [P, T], U8)
+        w3_planes_in = sb("w3_planes_in", [P, H], U8)
+        for planes in (tab_planes, w2_planes, tab2_planes, w3_planes_in):
+            nc.vector.memset(planes[:].bitcast(I32), 0)
         ident = sb("ident", [P, P], F32)
         make_identity(nc, ident[:])
-        warm = sb("warm", [P, 1], F32)
-        nc.scalar.activation(warm[:], ident[:, 0:1], ACT.Abs_reciprocal_sqrt, bias=1.0)
 
         idx = load_list("idx", offs)
-        load_scales_side_by_side(tab_sc, tab_scales)
-        tab = [load_table_words("tab%d" % a, tab_words, a) for a in range(2)]
-        load_scales_side_by_side(w2_sc, w2_scales)
-        w2c = []
-
-        def load_w2(b, tag):
-            w2c.append(sb("w2c%d" % b, [P, 2, 2 * PASS], U8, tag=tag))
-            nc.sync.dma_start(
-                w2c[b][:].bitcast(I32),
-                w2_words[:, :, 2 * PASS * b : 2 * PASS * (b + 1)].bitcast(I32).rearrange("a p n -> p a n"),
-            )
-
-        load_w2(0, "w2c0")
-        w1_raw0 = load_rows(0, w1, 0, half_cols[0])
-        w1_late = []
+        load_planes_side_by_side(tab_planes, tab_scales)
+        tab = [load_table_words("tab%d" % a, tab_words, a) for a in range(PASSES)]
+        load_planes_side_by_side(w2_planes, w2_scales)
+        w2_codes = [load_w2(0, None)]
+        load_k_rows(raw[0], w1, 0, cols512[0])
+        w1_parts = [sb("w1_part%d" % h, [P, PACK, PASS // 2], F32) for h in range(2)]
         for h in range(2):
-            piece = sb("w1_late%d" % h, [P, PACK, PASS // 2], F32)
-            nc.sync.dma_start(
-                piece[:], w1[PASS : 2 * PASS, PASS // 2 * h : PASS // 2 * (h + 1)].rearrange("(p j) c -> p j c", j=PACK)
-            )
-            w1_late.append(piece)
+            load_k_rows(w1_parts[h], w1, 1, slice(PASS // 2 * h, PASS // 2 * (h + 1)))
         idx3 = load_list("idx3", offs3)
         wg1_sb = sb("wg1_sb", [P, PACK, S], F32)
         load_cell_weights(wg1_sb, wg1, 0)
-        load_w2(1, "w1_late0")
-        w4_raw = []
-        for a in range(2):
+        w2_codes.append(load_w2(1, "w1_part0"))
+        for a in range(PASSES):
             load_cell_weights(wg1_sb, wg1, 1 + a)
-            w4_raw.append(load_rows(2 + a, w4, a, half_cols[0]))
+            load_k_rows(raw[PASSES + a], w4, a, cols512[0])
 
-        v, v_sc = [], []
-        for a in range(2):
-            v_sc.append(gather("v_sc%d" % a, tab_sc[:, T * a : T * (a + 1)], idx, U8))
-            v.append(gather("v%d" % a, tab[a][:], idx, U32))
+        v = []
+        for a in range(PASSES):
+            scales = gather("v_scales%d" % a, tab_planes[:, T * a : T * (a + 1)], idx, U8)
+            v.append((gather("v_codes%d" % a, tab[a][:], idx, U32)[:], scales[:]))
 
         idx2 = load_list("idx2", offs2)
-        load_scales_stacked(tab2_sc, tab2_scales)
-        tab2 = [load_table_words("tab2_%d" % a, tab2_words, a) for a in range(2)]
-        load_scales_stacked(w3_sc, w3_scales)
-        w3_raw = sb("w3_raw", [P, 2, H], I32)
-        nc.sync.dma_start(w3_raw[:], w3_words.rearrange("a p c i -> p a (c i)").bitcast(I32))
-        load_cell_weights(wg1_sb, wg1, PACK - 1)
+        load_planes_stacked(tab2_planes, tab2_scales)
+        tab2 = [load_table_words("tab2_%d" % a, tab2_words, a) for a in range(PASSES)]
+        load_planes_stacked(w3_planes_in, w3_scales)
+        w3_codes_in = sb("w3_codes_in", [P, PASSES, H], I32)
+        nc.sync.dma_start(w3_codes_in[:], w3_words.rearrange("a p c i -> p a (c i)").bitcast(I32))
+        load_cell_weights(wg1_sb, wg1, LAST)
         idx4 = load_list("idx4", offs4)
         wg2_sb = sb("wg2_sb", [P, PACK, S], F32)
 
-        roots = [sb("root%d" % b, [P, PACK, PACK, P], F32) for b in range(HALVES)]
+        squares = [sb("squares%d" % b, [P, PACK, PACK, P], F32) for b in range(HALVES)]
 
         def shear(b):
-            for a in range(2):
+            for a in range(PASSES):
+                lo = H * a + PASS * b
                 for c in range(PACK):
-                    mm(bank(c)[:], v[a][:, col128[c]].bitcast(FP8X4), v_sc[a][:, col128[c]],
-                       w2c[b][:, a, :].bitcast(FP4X4),
-                       w2_sc[:, H * a + PASS * b : H * a + PASS * (b + 1)], a == 0, a == 1)
+                    mm(banks[c][:], v[a][0][:, cols128[c]].bitcast(FP8X4), v[a][1][:, cols128[c]],
+                       w2_codes[b][:, a, :].bitcast(FP4X4), w2_planes[:, lo : lo + PASS], a == 0, a == PASSES - 1)
 
-        def square_shear(b, ts):
-            for c in range(PACK):
+        def square_shear(b, slots, entry_blocks):
+            for c in entry_blocks:
                 nc.scalar.activation(
-                    roots[b][:, ts, c, :].rearrange("p t (y x) -> p t y x", x=RUN),
-                    bank(c)[:].rearrange("p (y t x) -> p t y x", t=PACK, x=RUN)[:, ts, :, :],
+                    squares[b][:, slots, c, :].rearrange("p t (y x) -> p t y x", x=RUN),
+                    banks[c][:].rearrange("p (y t x) -> p t y x", t=PACK, x=RUN)[:, slots, :, :],
                     ACT.Square,
                 )
 
+        def slot_squares(b, t):
+            return squares[b][:, t, :, :].rearrange("p c m -> p (c m)")
+
+        def inverse_root(b, t, root, cols):
+            nc.scalar.activation(root[:, cols], slot_squares(b, t)[:, cols], ACT.Abs_reciprocal_sqrt, bias=1.0)
+
         def damping(b, t, root, turned):
-            squares = roots[b][:, t, :, :].rearrange("p c m -> p (c m)")
-            nc.scalar.activation(root, squares, ACT.Abs_reciprocal_sqrt, bias=1.0)
             for c in range(PACK):
-                nc.tensor.transpose(turned[:, col128[c]], root[:, col128[c]], ident[:])
-            damp = damp_ring[(PACK * b + t) % 6]
+                nc.tensor.transpose(turned[:, cols128[c]], root[:, cols128[c]], ident[:])
+            damp = damp_ring[(PACK * b + t) % RINGS]
             nc.scalar.activation(damp[:], turned[:], ACT.Square)
             return damp
 
-        def drive(w1q, damp, t, h1):
-            acc = bank(4 + t)
-            for a in range(2):
-                mm(acc[:], w1q[a][0][:, col128[t]].bitcast(FP8X4), w1q[a][1][:, col128[t]],
-                   v[a][:].bitcast(FP8X4), v_sc[a][:], a == 0, a == 1)
+        def root_and_damping(b, t, root, turned):
+            inverse_root(b, t, root, slice(0, S))
+            return damping(b, t, root, turned)
+
+        def drive(w1q, damp, t, h1, acc):
+            for a in range(PASSES):
+                mm_fp8(acc, w1q[a], cols128[t], v[a], a == 0, a == PASSES - 1)
             nc.vector.tensor_tensor(h1, acc[:], damp[:], MULT)
 
-        def put_drive(page, h1, t):
-            nc.vector.tensor_tensor(page[:].indirect(idx3[:]), h1, wg1_sb[:, t, :], MULT)
-
-        def cast_first_stage(name, slot, raw, scale):
-            grouped, dst, src = first_stage_views(slot, raw)
-            if scale == 1.0:
-                nc.scalar.copy(dst, src)
-            else:
-                for t in range(PACK):
-                    nc.scalar.activation(dst[:, t, :, :, :], src[:, t, :, :, :], ACT.Copy, scale=scale)
-            return quantize(name, grouped[:])
-
-        pages = [[page_ring[(PACK * b + t) % 6] for t in range(PACK)] for b in range(HALVES)]
-        shear(0)
-        square_shear(0, slice(0, 1))
-        in_place = [roots[0][:, t, :, :].rearrange("p c m -> p (c m)") for t in range(PACK)]
-        damp0 = [damping(0, 0, in_place[0], bank(7))]
-        square_shear(0, slice(1, PACK))
-
-        grouped, dst, src = first_stage_views(0, w1_raw0)
-        nc.vector.tensor_copy(dst, src)
-        w1q = [quantize("w1_00", grouped[:])]
-        grouped = grouped_ring[1]
-        for h in range(2):
-            nc.vector.tensor_copy(
-                grouped[:].rearrange("p (t y x j) -> p t y j x", t=PACK, x=RUN, j=PACK)[:, :, 16 * h : 16 * (h + 1), :, :],
-                w1_late[h][:].rearrange("p j (y t x) -> p t y j x", t=PACK, x=RUN),
-            )
-        codes = sb("w1_01_codes", [P, PASS], U32)
-        scales = sb("w1_01_scales", [P, PASS], U8)
-        for lo, hi in ((0, 1), (1, 2), (2, 4)):
-            quantize(None, grouped[:, PASS * lo : PASS * hi], codes[:, P * lo : P * hi], scales[:, P * lo : P * hi])
-        w1q.append((codes[:], scales[:]))
-        for t in range(PACK - 1):
-            drive(w1q, damp0[t], t, stream[t % 2][:])
-            if t == 0:
-                damp0.extend([damping(0, later, in_place[later], bank(4)) for later in range(1, PACK)])
-            put_drive(pages[0][t], stream[t % 2][:], t)
-
-        shear(1)
-        square_shear(1, slice(0, PACK))
-
-        v2_sc = gather("v2_sc", tab2_sc[:], idx2, U8)
-        v2 = [gather("v2_%d" % a, tab2[a][:], idx2, U32) for a in range(2)]
-
-        w3s = sb("w3s", [P, H], U8)
-        nc.vector.tensor_copy(
-            w3s[:].bitcast(I32).rearrange("p (b t y) -> p b t y", b=HALVES, t=PACK),
-            w3_sc[:].bitcast(I32).rearrange("p (b y t) -> p b t y", b=HALVES, t=PACK),
-        )
-        w3c = sb("w3c", [P, 2 * H], I32)
-        nc.vector.tensor_copy(
-            w3c[:].rearrange("p (g t y x) -> p g t y x", g=2 * HALVES, t=PACK, x=RUN),
-            w3_raw[:].rearrange("p a (b y t x) -> p (a b) t y x", b=HALVES, t=PACK, x=RUN),
-        )
+        def scatter_h1(b, t, h1):
+            nc.vector.tensor_tensor(pages[b][t][:].indirect(idx3[:]), h1, wg1_sb[:, t, :], MULT)
 
         def exchange(b, w4q, t):
-            acc = bank(t)
-            for a in range(2):
-                lo = PASS * b + P * t
-                mm(acc[:], w3c[:, H * a + lo : H * a + lo + P].bitcast(FP8X4), w3s[4 * a : P, lo : lo + P],
-                   v2[a][:].bitcast(FP8X4), v2_sc[4 * a : P, :], a == 0, False)
-            for a in range(2):
-                mm(acc[:], w4q[a][0][:, col128[t]].bitcast(FP8X4), w4q[a][1][:, col128[t]],
-                   v[a][:].bitcast(FP8X4), v_sc[a][:], False, a == 1)
-            nc.scalar.copy(stream[t][:], acc[:])
+            lo = PASS * b + P * t
+            for a in range(PASSES):
+                mm(banks[t][:], w3_codes[:, H * a + lo : H * a + lo + P].bitcast(FP8X4),
+                   w3_planes[4 * a : P, lo : lo + P], v2_codes[a][:].bitcast(FP8X4), v2_planes[4 * a : P, :],
+                   a == 0, False)
+            for a in range(PASSES):
+                mm_fp8(banks[t], w4q[a], cols128[t], v[a], False, a == PASSES - 1)
+            nc.scalar.copy(stream[t][:], banks[t][:])
 
-        def put_exchange(page, t):
-            nc.vector.tensor_tensor(page[:].indirect(idx4[:]), stream[t][:], wg2_sb[:, t, :], MULT)
+        def scatter_h2(b, t):
+            nc.vector.tensor_tensor(pages[b][t][:].indirect(idx4[:]), stream[t][:], wg2_sb[:, t, :], MULT)
 
-        z_rows = sb("z_rows", [P, PACK * T2], BF16)[:].rearrange("p (c t m) -> p c t m", t=PACK, m=CHUNK)
-        ths = [raw_ring[3][:, 2 * i : 2 * i + 2, :].rearrange("p j c -> p (j c)") for i in range(2)]
+        shear(0)
+        square_shear(0, slice(0, 1), range(1))
+        inverse_root(0, 0, slot_squares(0, 0), cols128[0])
+        square_shear(0, slice(0, 1), range(1, PACK))
+        inverse_root(0, 0, slot_squares(0, 0), slice(P, S))
+        damp0 = [damping(0, 0, slot_squares(0, 0), banks[5])]
+        square_shear(0, slice(1, PACK), range(PACK))
 
-        def activate(page, b, t, chunks, th):
-            cols = slice(CHUNK * chunks.start, CHUNK * chunks.stop)
-            nc.scalar.activation(th[:, cols], page[:, cols], ACT.Tanh)
-            nc.scalar.activation(
-                z_rows[:, chunks, t, :], th[:, cols].rearrange("p (c m) -> p c m", m=CHUNK),
-                ACT.Copy, scale=gain_sb[:, b, t, 0:1],
+        nc.vector.tensor_copy(words_view(grouped[0]), rows_view(raw[0]))
+        w1q = [quantize("w1_00", grouped[0][:])]
+        part_y = P // RUN // 2
+        for h in range(2):
+            nc.vector.tensor_copy(
+                words_view(grouped[1])[:, :, part_y * h : part_y * (h + 1), :, :], rows_view(w1_parts[h])
             )
-
-        def weave_views(grouped, chunk):
-            return (
-                grouped.rearrange("p (c i t) -> p c t i", t=PACK, i=RUN),
-                z_rows[:, chunk, :, :].rearrange("p t (c i) -> p c t i", i=RUN),
+        w1_codes = sb("w1_01_codes", [P, PASS], U32)
+        w1_scales = sb("w1_01_scales", [P, PASS], U8)
+        for lo, hi in ((0, 1), (1, 2), (2, PACK)):
+            quantize_into(
+                w1_codes[:, P * lo : P * hi], w1_scales[:, P * lo : P * hi], grouped[1][:, PASS * lo : PASS * hi]
             )
+        w1q.append((w1_codes[:], w1_scales[:]))
 
-        w4q = [cast_first_stage("w4_0%d" % a, 2 + a, w4_raw[a], -1.0) for a in range(2)]
-        damp1 = [damping(1, t, raw_ring[3][:, t, :], bank(4 + t % 3)) for t in range(PACK)]
-        held = sb("held", [P, S], F32, tag="w3_raw")[:]
-        drive(w1q, damp0[PACK - 1], PACK - 1, held)
-        put_drive(pages[0][PACK - 1], held, PACK - 1)
+        drive(w1q, damp0[0], 0, stream[0][:], banks[4])
+        damp0.extend([root_and_damping(0, t, slot_squares(0, t), banks[4]) for t in range(1, PACK)])
+        scatter_h1(0, 0, stream[0][:])
+        for t in range(1, LAST):
+            drive(w1q, damp0[t], t, stream[t % 2][:], banks[4 + t % 2])
+            scatter_h1(0, t, stream[t % 2][:])
 
-        gain_sb = sb("gain_sb", [P, HALVES, PACK, 8], F32)
+        shear(1)
+        square_shear(1, slice(0, PACK), range(PACK))
+
+        v2_planes = gather("v2_planes", tab2_planes[:], idx2, U8)
+        v2_codes = [gather("v2_codes%d" % a, tab2[a][:], idx2, U32) for a in range(PASSES)]
+
+        w3_planes = sb("w3_planes", [P, H], U8)
+        nc.vector.tensor_copy(
+            w3_planes[:].bitcast(I32).rearrange("p (b t y) -> p b t y", b=HALVES, t=PACK),
+            w3_planes_in[:].bitcast(I32).rearrange("p (b y t) -> p b t y", b=HALVES, t=PACK),
+        )
+        w3_codes = sb("w3_codes", [P, PASSES * H], I32)
+        nc.vector.tensor_copy(
+            w3_codes[:].rearrange("p (g t y x) -> p g t y x", g=PASSES * HALVES, t=PACK, x=RUN),
+            w3_codes_in[:].rearrange("p a (b y t x) -> p (a b) t y x", b=HALVES, t=PACK, x=RUN),
+        )
+
+        w4q = [quantize_negated_w4(0, a, tag="table%d" % a) for a in range(PASSES)]
+        damp1 = [root_and_damping(1, t, raw[3][:, t, :], banks[6 + t % 2]) for t in range(PACK)]
+        h1_last = sb("h1_last", [P, S], F32, tag="w3_codes_in")
+        drive(w1q, damp0[LAST], LAST, h1_last[:], banks[5])
+        scatter_h1(0, LAST, h1_last[:])
+
+        gain_sb = sb("gain_sb", [P, HALVES, PACK, GAIN_PITCH], F32)
         gain_rows = gain.rearrange("(b y t x o) -> b t y x o", b=HALVES, t=PACK, x=RUN, o=1)
-        second = []
         for t, w in enumerate((w1, w1, w4, w4)):
-            second.append(load_rows(t, w, t % 2, half_cols[1]))
             load_cell_weights(wg2_sb, wg2, t)
+            load_k_rows(raw[t], w, t % PASSES, cols512[1])
         with nc.allow_non_contiguous_dma(reason="one gain value for each partition"):
             for b in range(HALVES):
                 for t in range(PACK):
                     nc.sync.dma_start(gain_sb[:, b, t, 0:1], gain_rows[b, t])
-        w1_raw, w4_raw = second[:2], second[2:]
+
         for t in range(PACK):
             exchange(0, w4q, t)
-        w1q = [cast_first_stage("w1_1%d" % a, a, w1_raw[a], 1.0) for a in range(2)]
-        wo_raw = raw_ring[0:HALVES]
+        w1q = []
+        for a, engine_copy in enumerate((nc.scalar.copy, nc.vector.tensor_copy)):
+            engine_copy(words_view(grouped[a]), rows_view(raw[a]))
+            w1q.append(quantize("w1_1%d" % a, grouped[a][:]))
         for b in range(HALVES):
             for t in range(PACK):
                 nc.sync.dma_start(
-                    wo_raw[b][:, t, :],
-                    wo[PASS * b : PASS * (b + 1), :].rearrange("(y t x) n -> t y x n", t=PACK, x=RUN)[t],
+                    raw[b][:, t, :], wo[cols512[b], :].rearrange("(y t x) n -> t y x n", t=PACK, x=RUN)[t]
                 )
         for t in range(PACK):
-            put_exchange(pages[0][t], t)
-        w4q = [cast_first_stage("w4_1%d" % a, 2 + a, w4_raw[a], -1.0) for a in range(2)]
-        for t in range(PACK):
-            activate(pages[0][t], 0, t, slice(0, T2 // CHUNK), ths[t % 2])
+            scatter_h2(0, t)
+        w4q = [quantize_negated_w4(1, a) for a in range(PASSES)]
 
-        h1 = [grouped_ring[3][:, 2 * S * i : 2 * S * (i + 1)].bitcast(F32) for i in range(2)]
-        for pair in range(2):
-            for t in (2 * pair, 2 * pair + 1):
-                drive(w1q, damp1[t], t, h1[t % 2])
-            for t in (2 * pair, 2 * pair + 1):
-                put_drive(pages[1][t], h1[t % 2], t)
+        chunks = T2 // CHUNK
+        z_rows = sb("z_rows", [P, PACK * T2], BF16)[:].rearrange("p (c t m) -> p c t m", t=PACK, m=CHUNK)
+        tanh_out = [raw[3][:, 2 * i : 2 * i + 2, :].rearrange("p j c -> p (j c)") for i in range(2)]
 
-        z0 = []
-        for mh in range(2):
-            grouped = grouped_ring[mh]
-            for c in range(2):
-                dst, src = weave_views(grouped[:, PACK * CHUNK * c : PACK * CHUNK * (c + 1)], 2 * mh + c)
-                nc.scalar.copy(dst, src)
-            if mh == 0:
-                z0.append(quantize("z00", grouped[:]))
-        for t in range(PACK - 1):
-            exchange(1, w4q, t)
-        woq = []
-        wo_grouped = sb("wo_grouped", [P, HALVES * PACK * N], BF16, tag="w3_raw")
-        for b in range(HALVES):
-            grouped = wo_grouped[:, PACK * N * b : PACK * N * (b + 1)]
-            nc.scalar.copy(
-                grouped.rearrange("p (c i t) -> p c t i", t=PACK, i=RUN),
-                wo_raw[b][:].rearrange("p t (c i) -> p c t i", i=RUN),
+        def activate(b, t, first, count, th):
+            cols = slice(CHUNK * first, CHUNK * (first + count))
+            nc.scalar.activation(th[:, cols], pages[b][t][:, cols], ACT.Tanh)
+            nc.scalar.activation(
+                z_rows[:, first : first + count, t, :], th[:, cols].rearrange("p (c m) -> p c m", m=CHUNK),
+                ACT.Copy, scale=gain_sb[:, b, t, 0:1],
             )
-            if b == 0:
-                woq.append(quantize("wo0", grouped))
 
-        exchange(1, w4q, PACK - 1)
+        def interleave_z(engine_copy, tile, chunk):
+            lo = PACK * CHUNK * (chunk % 2)
+            interleave(engine_copy, tile[:, lo : lo + PACK * CHUNK], z_rows[:, chunk, :, :])
+
         for t in range(PACK):
-            put_exchange(pages[1][t], t)
+            activate(0, t, 0, chunks, tanh_out[t % 2])
+
+        h1_pair = [grouped[3][:, 2 * S * i : 2 * S * (i + 1)].bitcast(F32) for i in range(2)]
+        for pair in (range(0, 2), range(2, PACK)):
+            for t in pair:
+                drive(w1q, damp1[t], t, h1_pair[t % 2], banks[4 + t])
+            for t in pair:
+                scatter_h1(1, t, h1_pair[t % 2])
+
+        for chunk in (0, 1):
+            interleave_z(nc.scalar.copy, grouped[0], chunk)
+        z0q = [quantize("z00", grouped[0][:])]
+        for chunk in (2, 3):
+            interleave_z(nc.scalar.copy, grouped[1], chunk)
+        for t in range(LAST):
+            exchange(1, w4q, t)
+        wo_words = [
+            sb("wo_words0", [P, PACK * N], BF16, tag="w3_codes_in"),
+            sb("wo_words1", [P, PACK * N], BF16),
+        ]
+        interleave(nc.scalar.copy, wo_words[0][:], raw[0][:])
+        woq = [quantize("wo0", wo_words[0][:])]
+        interleave(nc.scalar.copy, wo_words[1][:], raw[1][:])
+        exchange(1, w4q, LAST)
+        for t in range(PACK):
+            scatter_h2(1, t)
 
         late_codes = sb("late_codes", [P, 2 * PASS], U32, tag="wg2_sb")
         late_scales = sb("late_scales", [P, 2 * PASS], U8)
-        z0.append(quantize(None, grouped_ring[1][:], late_codes[:, half_cols[0]], late_scales[:, half_cols[0]]))
-        woq.append(quantize(None, wo_grouped[:, PACK * N :], late_codes[:, half_cols[1]], late_scales[:, half_cols[1]]))
-        accs = {}
-        for mh in range(2):
-            for n in range(PACK):
-                accs[mh, n] = bank(4 * (1 - mh) + n)
-                mm(accs[mh, n][:], woq[0][0][:, col128[n]].bitcast(FP8X4), woq[0][1][:, col128[n]],
-                   z0[mh][0].bitcast(FP8X4), z0[mh][1], True, False)
+        z0q.append(quantize_into(late_codes[:, cols512[0]], late_scales[:, cols512[0]], grouped[1][:]))
+        woq.append(quantize_into(late_codes[:, cols512[1]], late_scales[:, cols512[1]], wo_words[1][:]))
 
-        for t in range(PACK - 1):
-            activate(pages[1][t], 1, t, slice(0, T2 // CHUNK), ths[0])
-        for mh in range(2):
-            grouped = grouped_ring[2]
-            for c in range(PASS // CHUNK):
-                chunk = 2 * mh + c
-                activate(pages[1][PACK - 1], 1, PACK - 1, slice(chunk, chunk + 1), ths[0])
-                dst, src = weave_views(grouped[:, PACK * CHUNK * c : PACK * CHUNK * (c + 1)], chunk)
-                nc.vector.tensor_copy(dst, src)
-            codes, scales = quantize("z1%d" % mh, grouped[:])
+        accs = [banks[PACK:], banks[:PACK]]
+        for u in range(2):
             for n in range(PACK):
-                mm(accs[mh, n][:], woq[1][0][:, col128[n]].bitcast(FP8X4), woq[1][1][:, col128[n]],
-                   codes.bitcast(FP8X4), scales, False, True)
-        for mh in range(2):
-            result = sb("result%d" % mh, [P, PACK, PASS], F32, tag="table%d" % mh)
+                mm_fp8(accs[u][n], woq[0], cols128[n], z0q[u], True, False)
+
+        for t in range(LAST):
+            activate(1, t, 0, chunks, tanh_out[0])
+        for u in range(2):
+            for chunk in (2 * u, 2 * u + 1):
+                activate(1, LAST, chunk, 1, tanh_out[0])
+                interleave_z(nc.vector.tensor_copy, grouped[2], chunk)
+            z1q = quantize("z1%d" % u, grouped[2][:])
             for n in range(PACK):
-                if mh == 1 and n % 2 == 1:
-                    nc.vector.tensor_copy(result[:, n, :], accs[mh, n][:])
-                else:
-                    nc.scalar.copy(result[:, n, :], accs[mh, n][:])
-                nc.sync.dma_start(out[col128[n], half_cols[mh]], result[:, n, :])
+                mm_fp8(accs[u][n], woq[1], cols128[n], z1q, False, True)
+        for u in range(2):
+            result = sb("result%d" % u, [P, PACK, PASS], F32, tag="table%d" % u)
+            for n in range(PACK):
+                engine_copy = nc.vector.tensor_copy if u == 1 and n % 2 == 1 else nc.scalar.copy
+                engine_copy(result[:, n, :], accs[u][n][:])
+                nc.sync.dma_start(out[cols128[n], cols512[u]], result[:, n, :])

from contextlib import ExitStack

import concourse.mybir as mybir
from concourse.masks import make_identity

K, T, S, T2, H, N = 1024, 2048, 512, 1024, 1024, 512
FLOPS = 2 * (4 * K * H * S + H * N * T2)

F32 = mybir.dt.float32
BF16 = mybir.dt.bfloat16
I32 = mybir.dt.int32
U32 = mybir.dt.uint32
U16 = mybir.dt.uint16
U8 = mybir.dt.uint8
FP8X4 = mybir.dt.float8_e4m3fn_x4
FP4X4 = mybir.dt.float4_e2m1fn_x4
ACT = mybir.ActivationFunctionType
MULT = mybir.AluOpType.mult

P = 128
PACK = 4
PASS = P * PACK
PASSES = K // PASS
HALVES = H // PASS
RUN = 4
CHUNK = 256
LAST = PACK - 1
QUADRANTS = (0, 2, 1, 3)
STAGES = 4
RINGS = 6
GAIN_PITCH = 8


def tile_list_tokamak_edge_weave_kernel(
    tc, tab_words, tab_scales, tab2_words, tab2_scales, offs, offs2, offs3, offs4,
    w1, w2_words, w2_scales, w3_words, w3_scales, w4, wg1, wg2, gain, wo, out,
):
    nc = tc.nc
    with ExitStack() as ctx:
        lists = ctx.enter_context(tc.tile_pool(name="lists", bufs=1))
        keep = ctx.enter_context(tc.tile_pool(name="keep", bufs=1))
        psum = ctx.enter_context(tc.psum_pool(name="psum", bufs=1))

        def sb(name, shape, dtype, tag=None):
            return keep.tile(shape, dtype, name=name, tag=tag or name, align_bytes=64)

        banks = [psum.tile([P, PASS], F32, name="bank%d" % i) for i in range(8)]
        raw = [sb("raw%d" % i, [P, PACK, PASS], F32) for i in range(STAGES)]
        grouped = [sb("grouped%d" % i, [P, PACK * PASS], BF16) for i in range(STAGES)]
        stream = [sb("stream%d" % i, [P, S], F32) for i in range(PACK)]
        damp_ring = [sb("damp%d" % i, [P, S], F32) for i in range(RINGS)]
        page_ring = [sb("page%d" % i, [P, T2], F32) for i in range(RINGS)]
        pages = [[page_ring[(PACK * b + t) % RINGS] for t in range(PACK)] for b in range(HALVES)]

        cols512 = [slice(PASS * i, PASS * (i + 1)) for i in range(2)]
        cols128 = [slice(P * i, P * (i + 1)) for i in range(PACK)]

        def load_list(name, offsets):
            tile = lists.tile([P, S // 16], U16, name=name)
            nc.sync.dma_start(tile[:], offsets)
            return tile

        def load_table_words(name, words, a):
            tile = sb(name, [P, T], U32, tag="table%d" % a)
            nc.sync.dma_start(tile[:].bitcast(I32), words[a].rearrange("p n i -> p (n i)").bitcast(I32))
            return tile

        def load_planes_side_by_side(tile, scales):
            for q in QUADRANTS:
                nc.sync.dma_start(
                    tile[32 * q : 32 * q + 4, :].bitcast(I32).rearrange("r (a n) -> r a n", a=PASSES),
                    scales[:, 4 * q : 4 * q + 4, :].bitcast(I32).rearrange("a r n -> r a n"),
                )

        def load_planes_stacked(tile, scales):
            for q in QUADRANTS:
                nc.sync.dma_start(
                    tile[32 * q : 32 * q + 8, :].bitcast(I32),
                    scales[:, 4 * q : 4 * q + 4, :].bitcast(I32),
                )

        def load_k_rows(tile, w, a, cols):
            nc.sync.dma_start(tile[:], w[cols512[a], cols].rearrange("(p j) c -> p j c", j=PACK))

        def load_cell_weights(tile, wg, t):
            for q in QUADRANTS:
                nc.sync.dma_start(
                    tile[32 * q : 32 * (q + 1), t, :], wg.rearrange("(y t x) j -> t y x j", t=PACK, x=RUN)[t]
                )

        def load_w2(b, tag):
            tile = sb("w2_codes%d" % b, [P, PASSES, 2 * PASS], U8, tag=tag)
            nc.sync.dma_start(
                tile[:].bitcast(I32),
                w2_words[:, :, 2 * PASS * b : 2 * PASS * (b + 1)].bitcast(I32).rearrange("a p n -> p a n"),
            )
            return tile

        def gather(name, window, offsets, dtype):
            picked = sb(name, [P, S], dtype)
            nc.vector.tensor_copy(picked[:], window.indirect(offsets[:]))
            return picked

        def quantize_into(codes, scales, values):
            nc.vector.quantize_mx(out=codes.bitcast(FP8X4), scales=scales, in_=values)
            return codes, scales

        def quantize(name, values, tag=None):
            codes = sb(name + "_codes", [P, PASS], U32, tag=tag)
            scales = sb(name + "_scales", [P, PASS], U8)
            return quantize_into(codes[:], scales[:], values)

        def mm(acc, lhs, lhs_scale, rhs, rhs_scale, start, stop):
            nc.tensor.matmul_mx(
                out=acc, lhsT=lhs, lhsT_scale=lhs_scale, rhs=rhs, rhs_scale=rhs_scale, start=start, stop=stop
            )

        def mm_fp8(acc, lhs, cols, rhs, start, stop):
            mm(acc[:], lhs[0][:, cols].bitcast(FP8X4), lhs[1][:, cols], rhs[0].bitcast(FP8X4), rhs[1], start, stop)

        def words_view(tile):
            return tile[:].rearrange("p (t y x j) -> p t y j x", t=PACK, x=RUN, j=PACK)

        def rows_view(tile):
            return tile[:].rearrange("p j (y t x) -> p t y j x", t=PACK, x=RUN)

        def quantize_negated_w4(b, a, tag=None):
            stage = PASSES + a
            for t in range(PACK):
                nc.scalar.activation(
                    words_view(grouped[stage])[:, t, :, :, :], rows_view(raw[stage])[:, t, :, :, :], ACT.Copy, scale=-1.0
                )
            return quantize("w4_%d%d" % (b, a), grouped[stage][:], tag=tag)

        def interleave(engine_copy, words, rows):
            engine_copy(
                words.rearrange("p (c i t) -> p c t i", t=PACK, i=RUN), rows.rearrange("p t (c i) -> p c t i", i=RUN)
            )

        tab_planes = sb("tab_planes", [P, PASSES * T], U8)
        w2_planes = sb("w2_planes", [P, PASSES * H], U8)
        tab2_planes = sb("tab2_planes", [P, T], U8)
        w3_planes_in = sb("w3_planes_in", [P, H], U8)
        for planes in (tab_planes, w2_planes, tab2_planes, w3_planes_in):
            nc.vector.memset(planes[:].bitcast(I32), 0)
        ident = sb("ident", [P, P], F32)
        make_identity(nc, ident[:])

        idx = load_list("idx", offs)
        load_planes_side_by_side(tab_planes, tab_scales)
        tab = [load_table_words("tab%d" % a, tab_words, a) for a in range(PASSES)]
        load_planes_side_by_side(w2_planes, w2_scales)
        w2_codes = [load_w2(0, None)]
        load_k_rows(raw[0], w1, 0, cols512[0])
        w1_parts = [sb("w1_part%d" % h, [P, PACK, PASS // 2], F32) for h in range(2)]
        for h in range(2):
            load_k_rows(w1_parts[h], w1, 1, slice(PASS // 2 * h, PASS // 2 * (h + 1)))
        idx3 = load_list("idx3", offs3)
        wg1_sb = sb("wg1_sb", [P, PACK, S], F32)
        load_cell_weights(wg1_sb, wg1, 0)
        w2_codes.append(load_w2(1, "w1_part0"))
        for a in range(PASSES):
            load_cell_weights(wg1_sb, wg1, 1 + a)
            load_k_rows(raw[PASSES + a], w4, a, cols512[0])

        v = []
        for a in range(PASSES):
            scales = gather("v_scales%d" % a, tab_planes[:, T * a : T * (a + 1)], idx, U8)
            v.append((gather("v_codes%d" % a, tab[a][:], idx, U32)[:], scales[:]))

        idx2 = load_list("idx2", offs2)
        load_planes_stacked(tab2_planes, tab2_scales)
        tab2 = [load_table_words("tab2_%d" % a, tab2_words, a) for a in range(PASSES)]
        load_planes_stacked(w3_planes_in, w3_scales)
        w3_codes_in = sb("w3_codes_in", [P, PASSES, H], I32)
        nc.sync.dma_start(w3_codes_in[:], w3_words.rearrange("a p c i -> p a (c i)").bitcast(I32))
        load_cell_weights(wg1_sb, wg1, LAST)
        idx4 = load_list("idx4", offs4)
        wg2_sb = sb("wg2_sb", [P, PACK, S], F32)

        squares = [sb("squares%d" % b, [P, PACK, PACK, P], F32) for b in range(HALVES)]

        def shear(b):
            for a in range(PASSES):
                lo = H * a + PASS * b
                for c in range(PACK):
                    mm(banks[c][:], v[a][0][:, cols128[c]].bitcast(FP8X4), v[a][1][:, cols128[c]],
                       w2_codes[b][:, a, :].bitcast(FP4X4), w2_planes[:, lo : lo + PASS], a == 0, a == PASSES - 1)

        def square_shear(b, slots, entry_blocks):
            for c in entry_blocks:
                nc.scalar.activation(
                    squares[b][:, slots, c, :].rearrange("p t (y x) -> p t y x", x=RUN),
                    banks[c][:].rearrange("p (y t x) -> p t y x", t=PACK, x=RUN)[:, slots, :, :],
                    ACT.Square,
                )

        def slot_squares(b, t):
            return squares[b][:, t, :, :].rearrange("p c m -> p (c m)")

        def inverse_root(b, t, root, cols):
            nc.scalar.activation(root[:, cols], slot_squares(b, t)[:, cols], ACT.Abs_reciprocal_sqrt, bias=1.0)

        def damping(b, t, root, turned):
            for c in range(PACK):
                nc.tensor.transpose(turned[:, cols128[c]], root[:, cols128[c]], ident[:])
            damp = damp_ring[(PACK * b + t) % RINGS]
            nc.scalar.activation(damp[:], turned[:], ACT.Square)
            return damp

        def root_and_damping(b, t, root, turned):
            inverse_root(b, t, root, slice(0, S))
            return damping(b, t, root, turned)

        def drive(w1q, damp, t, h1, acc):
            for a in range(PASSES):
                mm_fp8(acc, w1q[a], cols128[t], v[a], a == 0, a == PASSES - 1)
            nc.vector.tensor_tensor(h1, acc[:], damp[:], MULT)

        def scatter_h1(b, t, h1):
            nc.vector.tensor_tensor(pages[b][t][:].indirect(idx3[:]), h1, wg1_sb[:, t, :], MULT)

        def exchange(b, w4q, t):
            lo = PASS * b + P * t
            for a in range(PASSES):
                mm(banks[t][:], w3_codes[:, H * a + lo : H * a + lo + P].bitcast(FP8X4),
                   w3_planes[4 * a : P, lo : lo + P], v2_codes[a][:].bitcast(FP8X4), v2_planes[4 * a : P, :],
                   a == 0, False)
            for a in range(PASSES):
                mm_fp8(banks[t], w4q[a], cols128[t], v[a], False, a == PASSES - 1)
            nc.scalar.copy(stream[t][:], banks[t][:])

        def scatter_h2(b, t):
            nc.vector.tensor_tensor(pages[b][t][:].indirect(idx4[:]), stream[t][:], wg2_sb[:, t, :], MULT)

        shear(0)
        square_shear(0, slice(0, 1), range(1))
        inverse_root(0, 0, slot_squares(0, 0), cols128[0])
        square_shear(0, slice(0, 1), range(1, PACK))
        inverse_root(0, 0, slot_squares(0, 0), slice(P, S))
        damp0 = [damping(0, 0, slot_squares(0, 0), banks[5])]
        square_shear(0, slice(1, PACK), range(PACK))

        nc.vector.tensor_copy(words_view(grouped[0]), rows_view(raw[0]))
        w1q = [quantize("w1_00", grouped[0][:])]
        part_y = P // RUN // 2
        for h in range(2):
            nc.vector.tensor_copy(
                words_view(grouped[1])[:, :, part_y * h : part_y * (h + 1), :, :], rows_view(w1_parts[h])
            )
        w1_codes = sb("w1_01_codes", [P, PASS], U32)
        w1_scales = sb("w1_01_scales", [P, PASS], U8)
        for lo, hi in ((0, 1), (1, 2), (2, PACK)):
            quantize_into(
                w1_codes[:, P * lo : P * hi], w1_scales[:, P * lo : P * hi], grouped[1][:, PASS * lo : PASS * hi]
            )
        w1q.append((w1_codes[:], w1_scales[:]))

        drive(w1q, damp0[0], 0, stream[0][:], banks[4])
        damp0.extend([root_and_damping(0, t, slot_squares(0, t), banks[4]) for t in range(1, PACK)])
        scatter_h1(0, 0, stream[0][:])
        for t in range(1, LAST):
            drive(w1q, damp0[t], t, stream[t % 2][:], banks[4 + t % 2])
            scatter_h1(0, t, stream[t % 2][:])

        shear(1)
        square_shear(1, slice(0, PACK), range(PACK))

        v2_planes = gather("v2_planes", tab2_planes[:], idx2, U8)
        v2_codes = [gather("v2_codes%d" % a, tab2[a][:], idx2, U32) for a in range(PASSES)]

        w3_planes = sb("w3_planes", [P, H], U8)
        nc.vector.tensor_copy(
            w3_planes[:].bitcast(I32).rearrange("p (b t y) -> p b t y", b=HALVES, t=PACK),
            w3_planes_in[:].bitcast(I32).rearrange("p (b y t) -> p b t y", b=HALVES, t=PACK),
        )
        w3_codes = sb("w3_codes", [P, PASSES * H], I32)
        nc.vector.tensor_copy(
            w3_codes[:].rearrange("p (g t y x) -> p g t y x", g=PASSES * HALVES, t=PACK, x=RUN),
            w3_codes_in[:].rearrange("p a (b y t x) -> p (a b) t y x", b=HALVES, t=PACK, x=RUN),
        )

        w4q = [quantize_negated_w4(0, a, tag="table%d" % a) for a in range(PASSES)]
        damp1 = [root_and_damping(1, t, raw[3][:, t, :], banks[6 + t % 2]) for t in range(PACK)]
        h1_last = sb("h1_last", [P, S], F32, tag="w3_codes_in")
        drive(w1q, damp0[LAST], LAST, h1_last[:], banks[5])
        scatter_h1(0, LAST, h1_last[:])

        gain_sb = sb("gain_sb", [P, HALVES, PACK, GAIN_PITCH], F32)
        gain_rows = gain.rearrange("(b y t x o) -> b t y x o", b=HALVES, t=PACK, x=RUN, o=1)
        for t, w in enumerate((w1, w1, w4, w4)):
            load_cell_weights(wg2_sb, wg2, t)
            load_k_rows(raw[t], w, t % PASSES, cols512[1])
        with nc.allow_non_contiguous_dma(reason="one gain value for each partition"):
            for b in range(HALVES):
                for t in range(PACK):
                    nc.sync.dma_start(gain_sb[:, b, t, 0:1], gain_rows[b, t])

        for t in range(PACK):
            exchange(0, w4q, t)
        w1q = []
        for a, engine_copy in enumerate((nc.scalar.copy, nc.vector.tensor_copy)):
            engine_copy(words_view(grouped[a]), rows_view(raw[a]))
            w1q.append(quantize("w1_1%d" % a, grouped[a][:]))
        for b in range(HALVES):
            for t in range(PACK):
                nc.sync.dma_start(
                    raw[b][:, t, :], wo[cols512[b], :].rearrange("(y t x) n -> t y x n", t=PACK, x=RUN)[t]
                )
        for t in range(PACK):
            scatter_h2(0, t)
        w4q = [quantize_negated_w4(1, a) for a in range(PASSES)]

        chunks = T2 // CHUNK
        z_rows = sb("z_rows", [P, PACK * T2], BF16)[:].rearrange("p (c t m) -> p c t m", t=PACK, m=CHUNK)
        tanh_out = [raw[3][:, 2 * i : 2 * i + 2, :].rearrange("p j c -> p (j c)") for i in range(2)]

        def activate(b, t, first, count, th):
            cols = slice(CHUNK * first, CHUNK * (first + count))
            nc.scalar.activation(th[:, cols], pages[b][t][:, cols], ACT.Tanh)
            nc.scalar.activation(
                z_rows[:, first : first + count, t, :], th[:, cols].rearrange("p (c m) -> p c m", m=CHUNK),
                ACT.Copy, scale=gain_sb[:, b, t, 0:1],
            )

        def interleave_z(engine_copy, tile, chunk):
            lo = PACK * CHUNK * (chunk % 2)
            interleave(engine_copy, tile[:, lo : lo + PACK * CHUNK], z_rows[:, chunk, :, :])

        for t in range(PACK):
            activate(0, t, 0, chunks, tanh_out[t % 2])

        h1_pair = [grouped[3][:, 2 * S * i : 2 * S * (i + 1)].bitcast(F32) for i in range(2)]
        for pair in (range(0, 2), range(2, PACK)):
            for t in pair:
                drive(w1q, damp1[t], t, h1_pair[t % 2], banks[4 + t])
            for t in pair:
                scatter_h1(1, t, h1_pair[t % 2])

        for chunk in (0, 1):
            interleave_z(nc.scalar.copy, grouped[0], chunk)
        z0q = [quantize("z00", grouped[0][:])]
        for chunk in (2, 3):
            interleave_z(nc.scalar.copy, grouped[1], chunk)
        for t in range(LAST):
            exchange(1, w4q, t)
        wo_words = [
            sb("wo_words0", [P, PACK * N], BF16, tag="w3_codes_in"),
            sb("wo_words1", [P, PACK * N], BF16),
        ]
        interleave(nc.scalar.copy, wo_words[0][:], raw[0][:])
        woq = [quantize("wo0", wo_words[0][:])]
        interleave(nc.scalar.copy, wo_words[1][:], raw[1][:])
        exchange(1, w4q, LAST)
        for t in range(PACK):
            scatter_h2(1, t)

        late_codes = sb("late_codes", [P, 2 * PASS], U32, tag="wg2_sb")
        late_scales = sb("late_scales", [P, 2 * PASS], U8)
        z0q.append(quantize_into(late_codes[:, cols512[0]], late_scales[:, cols512[0]], grouped[1][:]))
        woq.append(quantize_into(late_codes[:, cols512[1]], late_scales[:, cols512[1]], wo_words[1][:]))

        accs = [banks[PACK:], banks[:PACK]]
        for u in range(2):
            for n in range(PACK):
                mm_fp8(accs[u][n], woq[0], cols128[n], z0q[u], True, False)

        for t in range(LAST):
            activate(1, t, 0, chunks, tanh_out[0])
        for u in range(2):
            for chunk in (2 * u, 2 * u + 1):
                activate(1, LAST, chunk, 1, tanh_out[0])
                interleave_z(nc.vector.tensor_copy, grouped[2], chunk)
            z1q = quantize("z1%d" % u, grouped[2][:])
            for n in range(PACK):
                mm_fp8(accs[u][n], woq[1], cols128[n], z1q, False, True)
        for u in range(2):
            result = sb("result%d" % u, [P, PACK, PASS], F32, tag="table%d" % u)
            for n in range(PACK):
                engine_copy = nc.vector.tensor_copy if u == 1 and n % 2 == 1 else nc.scalar.copy
                engine_copy(result[:, n, :], accs[u][n][:])
                nc.sync.dma_start(out[cols128[n], cols512[u]], result[:, n, :])
